import numpy as np, ml_dtypes
CORES = [2,3,42,43,82,83,122,123]
N = 8
import mx_ref
BF = ml_dtypes.bfloat16
def entries(a):
    return np.ascontiguousarray(a.T).reshape(-1)
def table(e):
    return np.ascontiguousarray(np.reshape(e, (-1, 16)).T).astype(np.int32)
def cols(t, e):
    v = np.concatenate([t.reshape(128, -1, 4), np.zeros((128, 1, 4), BF)], axis=1)
    return np.ascontiguousarray(v[:, e]).reshape(128, -1)
def f(rng, *shape):
    return mx_ref.flush((rng.standard_normal(shape, dtype=np.float32) * np.exp2(rng.integers(-2, 3, shape[:-1] + (1,)))).astype(BF))
def wide(rng, *shape, cols=0):
    v = rng.standard_normal(shape, dtype=np.float32) * np.exp2(rng.integers(-12, 13, shape)).astype(np.float32)
    if cols: v *= np.repeat(np.exp2(rng.integers(-cols, cols + 1, shape[:-2] + (1, shape[-1] // 4))) * (rng.random(shape[:-2] + (1, shape[-1] // 4)) > 0.0625), 4, axis=-1).astype(np.float32)
    return mx_ref.flush(v.astype(BF))
T, NA, S, CAPP = 512, 256, 512, 96
def lists(rng, most=0, inorder=False, big=None):
    c, m = [], []
    for r in range(N):
        n = np.zeros(N, int)
        n[rng.permutation(N)[:most]] = CAPP
        while n.sum() < S:
            q = rng.integers(0, N)
            if n[q] < CAPP: n[q] += 1
        used = np.concatenate([q * CAPP + rng.permutation(CAPP)[:n[q]] for q in range(N)])
        slots = np.full(N * CAPP, -1); slots[used] = rng.integers(0, T, S)
        o = np.sort(used) if inorder else rng.permutation(used)
        if big is not None:
            for i in range(S // 32):
                k = o[32 * i + rng.integers(0, 32)]; slots[k] = rng.choice(big[k // CAPP])
        c.append(table(slots)); m.append(table(o))
    return {"want": np.stack(c), "slot": np.stack(m)}
def setup_inputs(rng):
    return {"v": f(rng, N, 128, 4 * T), "a": f(rng, N, 128, 4 * NA), **lists(rng)}
def setup_inputs_full(rng):
    return {**setup_inputs(rng), **lists(rng, most=S // CAPP)}
def setup_inputs_sorted(rng):
    return {**setup_inputs(rng), **lists(rng, inorder=True)}
def setup_inputs_giant(rng):
    d = setup_inputs(rng); big = [rng.permutation(T)[:T // 32] for q in range(N)]
    x = d["v"].reshape(N, 128, T, 4)
    for q in range(N): x[q][:, big[q]] = (x[q][:, big[q]].astype(np.float32) * np.float32(2.0 ** 20)).astype(BF)
    d["v"] = x.reshape(N, 128, 4 * T)
    return {**d, **lists(rng, big=big)}
def setup_inputs_spread(rng):
    d = setup_inputs(rng); d["v"] = wide(rng, N, 128, 4 * T); d["a"] = wide(rng, N, 128, 4 * NA); return d
def check_inputs(d):
    b = []
    for r in range(N):
        c, m = entries(d["want"][r]), entries(d["slot"][r])
        if c.min() < -1 or c.max() >= T or (c >= 0).sum() != S: b.append("want")
        if m.min() < 0 or m.max() >= N * CAPP or len(set(m.tolist())) != S or (c[np.clip(m, 0, N * CAPP - 1)] < 0).any(): b.append("slot")
    return b
def ones(b):
    e = np.zeros((128, 128, 4), np.float32); e[np.arange(128), np.arange(128), b] = 1
    return e.reshape(128, 512).astype(BF)
def decode(q):
    return np.stack([mx_ref.matmul(mx_ref.quantize(ones(b)), q) for b in range(4)], axis=1).reshape(512, -1)
def reference(v, a, want, slot, own=None):
    h = np.zeros((N, 128, 2048), BF); y = np.zeros((N, 128, 4 * NA), np.float32)
    for r in range(N):
        c = entries(want[r])
        arrived = np.concatenate([decode(mx_ref.quantize(cols(v[q], c[q * CAPP:(q + 1) * CAPP]))) for q in range(N)], axis=1)
        H = arrived[:, entries(slot[r])].T
        h[r] = H.reshape(128, 4, 512).transpose(0, 2, 1).reshape(128, 2048).astype(BF)
    for r in range(N):
        t = h[r] if own is None else np.asarray(own["h"][r])
        for o in range(4):
            y[r][:, NA * o:NA * o + NA] = mx_ref.matmul(mx_ref.quantize(np.ascontiguousarray(t[:, 512 * o:512 * o + 512])), mx_ref.quantize(a[r]))
    return {"y": y, "h": h}

@@ -1,0 +1,321 @@
+from concourse.bass import DstId, RemoteDMATransfer
+from concourse.mybir import dt, AluOpType, ActivationFunctionType
+
+N, CAPP, NV, NA, S = 8, 96, 512, 256, 512
+W = N * CAPP
+LW = CAPP // 16
+COPY = ActivationFunctionType.Copy
+OWNAT = 1.5
+UORD = [0, 3, 2, 1]
+TAIL = "p0 L p1 t0 t1 e0V q0 m0 y0 e1 l2 q2 m2 q1 m1 y2 y1 l3 q3 m3 y3V"
+
+SCRATCH = {
+    "w32": ("sbuf", [128, N * LW], "int32"),
+    "w16": ("sbuf", [128, N * LW], "uint16"),
+    "lst": ("sbuf", [128, N * LW], "uint16"),
+    "s32": ("sbuf", [128, S // 16], "int32"),
+    "s16": ("sbuf", [128, S // 16], "uint16"),
+    "sl": ("sbuf", [128, S // 8], "uint16"),
+    "vt": ("sbuf", [128, 4 * NV], "bfloat16"),
+    "at": ("sbuf", [128, 4 * NA], "bfloat16"),
+    "aq": ("sbuf", [128, NA], "float8_e4m3fn_x4"),
+    "ap": ("sbuf", [128, NA], "uint8"),
+    "mi": ("sbuf", [128, 128], "float32"),
+    "pi": ("sbuf", [128, 16], "float32"),
+    "jt": ("sbuf", [128, 512], "bfloat16"),
+    "jl": ("sbuf", [128, 512], "bfloat16"),
+    "et": ("sbuf", [128, 2048], "bfloat16"),
+    "eq": ("sbuf", [128, 512], "float8_e4m3fn_x4"),
+    "ep": ("sbuf", [128, 512], "uint8"),
+    "ident": ("sbuf", [128, 128], "float32"),
+    "x0": ("sbuf", [128, 512], "bfloat16"),
+    "q0": ("sbuf", [128, 128], "float8_e4m3fn_x4"),
+    "p0": ("sbuf", [128, 128], "uint8"),
+    "cq": ("sbuf", [128, W], "float8_e4m3fn_x4"),
+    "cp": ("sbuf", [128, W], "uint8"),
+    "dw": ("sbuf", [128, 4 * W], "bfloat16"),
+    "gt": ("sbuf", [128, 2 * S], "float32"),
+    "gl": ("sbuf", [128, 2 * S], "bfloat16"),
+    "gm": ("sbuf", [128, 2 * S], "bfloat16"),
+    "ht": ("sbuf", [128, 4 * S], "bfloat16"),
+    "hq": ("sbuf", [128, S], "float8_e4m3fn_x4"),
+    "hp": ("sbuf", [128, S], "uint8"),
+    "yt": ("sbuf", [128, 4 * NA], "float32"),
+    "psu": ("psum", [128, 2048], "float32"),
+    "pst": ("psum", [128, 1024], "float32"),
+    "psy": ("psum", [128, 1024], "float32"),
+}
+for _k, _n in ((1, 2), (2, 3), (3, 2)):
+    SCRATCH["x%d" % _k] = ("sbuf", [128, 4 * CAPP * _n], "bfloat16")
+    SCRATCH["q%d" % _k] = ("sbuf", [128, CAPP * _n], "float8_e4m3fn_x4")
+    SCRATCH["p%d" % _k] = ("sbuf", [128, CAPP * _n], "uint8")
+NEV = 96
+SEMAPHORES = (["lst1", "lst2", "lst3", "loc"] + ["arr%d" % k for k in range(N // 2)] + ["dw%d" % k for k in range(4)]
+              + ["e%d" % k for k in range(NEV)])
+
+
+def relation(topo, a, b):
+    ca, cb = topo.chip(a), topo.chip(b)
+    return 2 if ca == cb else 1 if topo.same_plane(ca, cb) else 0
+
+
+def batches(topo, cores, r):
+    rel = [relation(topo, cores[r], c) for c in cores]
+    near = sorted([q for q in range(N) if q != r], key=lambda q: (q // 2 - r // 2) % (N // 2) * N + q)
+    far = [q for q in near if rel[q] == 0]
+    return [far[:2], far[2:] + [q for q in near if rel[q] == 2], [q for q in near if rel[q] == 1]]
+
+
+def peers(topo, cores, r):
+    return [q for b in batches(topo, cores, r) for q in b]
+
+
+def lanes(topo, cores, r, group):
+    off = [q for q in group if relation(topo, cores[r], cores[q]) < 2]
+    eng = topo.engines(cores[r], cores[off[0]])
+    wide = 1
+    while 2 * wide * len(off) <= len(eng):
+        wide *= 2
+    spare = (len(eng) - wide * len(off)) // wide
+    out, at = {}, 0
+    for k, q in enumerate(off):
+        n = 2 * wide if len(off) - k <= spare else wide
+        out[q] = eng[at:at + n]
+        at += n
+    for q in group:
+        if q not in out:
+            out[q] = [e for e in topo.engines(cores[r], cores[q]) if e not in eng][:2]
+    return out
+
+
+def rank_program(g, core, T, topo):
+    r = T.rank_of(core)
+    if r is None:
+        return
+    cores = list(T.cores)
+    V, A, P, Y = g.vector, g.scalar, g.tensor, g.sync
+    order = peers(topo, cores, r)
+    used, nloc = [0], [0]
+
+    def ev():
+        used[0] += 1
+        return T.sem["e%d" % (used[0] - 1)]
+
+    def copy(q, out, src, sem):
+        if q is V:
+            V.tensor_copy(out, src).then_inc(sem, 1)
+        else:
+            A.activation(out, src, COPY).then_inc(sem, 1)
+
+    def send(group, piece, sem_of):
+        eng = lanes(topo, cores, r, group)
+        tr = []
+        for q in group:
+            rid, pid, _ = topo.addr(cores[q])
+            src, dst = piece(q)
+            m = 0
+            for e in eng[q]:
+                m += 1 << e
+            tr.append(RemoteDMATransfer(dst_ids=[DstId(rid=rid, pnc=pid)], dma_engine_mask=m, remote_sem=sem_of(q),
+                                        src=src, dst=dst))
+            nloc[0] += len(eng[q])
+        g.remote_dma_fused(tr, local_sem=T.sem.loc)
+
+    def batch_of(s, q):
+        return [q in b for b in batches(topo, cores, s)].index(True)
+
+    e_w, e_v, e_s, e_a = ev(), ev(), ev(), ev()
+    for k in range(8):
+        (Y if k % 2 == 0 else A).dma_start(T.w32[16 * k:16 * k + 16, :], T.want[:]).then_inc(e_w, 16)
+    Y.dma_start(T.vt[:], T.v[:]).then_inc(e_v, 16)
+    for k in range(8):
+        Y.dma_start(T.s32[16 * k:16 * k + 16, :], T.slot[:]).then_inc(e_s, 16)
+    Y.dma_start(T.at[:], T.a[:]).then_inc(e_a, 16)
+
+    e_i, e_z, e_j, e_k = ev(), ev(), ev(), ev()
+    g.iota(T.mi[:], [[1, 128]], 0, 0, allow_small_or_imprecise_dtypes=True).then_inc(e_i, 1)
+    g.iota(T.pi[:], [[-32, 16]], 0, 4, allow_small_or_imprecise_dtypes=True).then_inc(e_i, 1)
+    V.memset(T.x0[:, 4 * CAPP:512], 0.0).then_inc(e_z, 1)
+    V.wait_ge(e_i, 2)
+    for t in range(4):
+        V.tensor_scalar(T.jt[:, t:512:4], T.mi[:], float(t), None, AluOpType.subtract).then_inc(e_j, 1)
+
+    e_c = ev()
+    V.wait_ge(e_w, 128)
+    V.tensor_scalar(T.w16[:], T.w32[:], 0.0, 4.0, AluOpType.max, AluOpType.mult).then_inc(e_c, 1)
+
+    def list_piece(q):
+        k = peers(topo, cores, q).index(r)
+        return T.w16[:, LW * q:LW * q + LW], T.lst[:, LW * k:LW * k + LW]
+
+    g.wait_ge(e_c, 1)
+    send(order, list_piece, lambda q: T.sem["lst%d" % (1 + batch_of(q, r))])
+
+    e_e, e_eq = ev(), ev()
+    V.wait_ge(e_j, 4)
+    for s in range(4):
+        V.tensor_scalar(T.jl[:, 128 * s:128 * s + 128], T.jt[:, 128 * s:128 * s + 128], 32.0 * s, None,
+                        AluOpType.add).then_inc(e_k, 1)
+    for o in range(2):
+        V.tensor_scalar(T.et[:, 512 * o:512 * o + 512], T.jt[:], T.pi[:, 4 * o:4 * o + 1], None,
+                        AluOpType.is_equal).then_inc(e_e, 1)
+    V.wait_ge(e_k, 4)
+    for b in range(2):
+        V.tensor_scalar(T.et[:, 1024 + 512 * b:1536 + 512 * b], T.jl[:], T.pi[:, 8 + b:9 + b], None,
+                        AluOpType.is_equal).then_inc(e_e, 1)
+    V.wait_ge(e_e, 4)
+    V.quantize_mx(T.eq[:], T.ep[:], T.et[:]).then_inc(e_eq, 1)
+
+    e_g0, e_q0, e_own = ev(), ev(), ev()
+    A.wait_ge(e_v, 16)
+    A.wait_ge(e_c, 1)
+    for t in range(4):
+        A.activation(T.x0[:, t:4 * CAPP:4], T.vt[:, t:4 * NV].indirect(T.w16[:, LW * r:LW * r + LW]), COPY).then_inc(e_g0, 1)
+    V.wait_ge(e_z, 1)
+    V.wait_ge(e_g0, 4)
+    V.quantize_mx(T.q0[:], T.p0[:], T.x0[:]).then_inc(e_q0, 1)
+    Y.wait_ge(e_q0, 1)
+    Y.dma_start(T.cq[:, CAPP * r:CAPP * r + CAPP].bitcast(dt.uint8), T.q0[:, 0:CAPP].bitcast(dt.uint8)).then_inc(e_own, 16)
+    Y.dma_start(T.cp[:, CAPP * r:CAPP * r + CAPP], T.p0[:, 0:CAPP]).then_inc(e_own, 16)
+
+    V.wait_ge(e_v, 16)
+    c0 = 0
+    for i, grp in enumerate(batches(topo, cores, r)):
+        x, qb, pb = T["x%d" % (i + 1)], T["q%d" % (i + 1)], T["p%d" % (i + 1)]
+        need = sum(len(lanes(topo, cores, s, peers(topo, cores, s))[r]) for s in grp)
+        n = CAPP * len(grp)
+        off = T.lst[:, LW * c0:LW * (c0 + len(grp))]
+        e_g, e_q = ev(), ev()
+        V.wait_ge(T.sem["lst%d" % (i + 1)], need)
+        A.wait_ge(T.sem["lst%d" % (i + 1)], need)
+        for t in range(4):
+            copy(V if t % 2 == 0 else A, x[:, t:4 * n:4], T.vt[:, t:4 * NV].indirect(off), e_g)
+        V.wait_ge(e_g, 4)
+        V.quantize_mx(qb[:], pb[:], x[:]).then_inc(e_q, 1)
+        g.wait_ge(e_q, 1)
+
+        def codes(q):
+            k = CAPP * grp.index(q)
+            return qb[:, k:k + CAPP].bitcast(dt.uint8), T.cq[:, CAPP * r:CAPP * r + CAPP].bitcast(dt.uint8)
+
+        def planes(q):
+            k = CAPP * grp.index(q)
+            return pb[:, k:k + CAPP], T.cp[:, CAPP * r:CAPP * r + CAPP]
+
+        send(grp, codes, lambda q: T.sem["arr%d" % (r // 2)])
+        send(grp, planes, lambda q: T.sem["arr%d" % (r // 2)])
+        c0 += len(grp)
+    g.wait_ge(T.sem.loc, nloc[0])
+
+    e_id, e_s16, e_sl, e_aq = ev(), ev(), ev(), ev()
+    V.tensor_scalar(T.ident[:], T.mi[:], 4.0, T.pi[:, 0:1], AluOpType.mult, AluOpType.is_equal).then_inc(e_id, 1)
+    V.wait_ge(e_s, 128)
+    V.tensor_copy(T.s16[:], T.s32[:]).then_inc(e_s16, 1)
+    for a in range(4):
+        for b in range(2):
+            V.tensor_scalar(T.sl[:, 16 * a + 8 * b:16 * a + 8 * b + 8], T.s32[:, 8 * a:8 * a + 8], float(b * W), None,
+                            AluOpType.add).then_inc(e_sl, 1)
+    V.wait_ge(e_a, 16)
+    V.quantize_mx(T.aq[:], T.ap[:], T.at[:]).then_inc(e_aq, 1)
+
+    PW = 2 * CAPP
+    pairs = sorted(range(N // 2), key=lambda k: OWNAT if k == r // 2 else batch_of(2 * k, r))
+    P.wait_ge(e_eq, 1)
+    for c, k in enumerate(pairs):
+        need = 0
+        for s in (2 * k, 2 * k + 1):
+            if s != r:
+                need += 2 * len(lanes(topo, cores, s, batches(topo, cores, s)[batch_of(s, r)])[r])
+        if k == r // 2:
+            P.wait_ge(e_own, 32)
+        P.wait_ge(T.sem["arr%d" % k], need)
+        for o in UORD:
+            e_u, e_d = ev(), T.sem["dw%d" % o]
+            if c:
+                P.wait_ge(e_d, c)
+            P.matmul_mx(T.psu[:, 512 * o:512 * o + PW], T.eq[:, 128 * o:128 * o + 128], T.ep[:, 128 * o:128 * o + 128],
+                        T.cq[:, PW * k:PW * k + PW], T.cp[:, PW * k:PW * k + PW], True, True).then_inc(e_u, 1)
+            q = V if o % 2 == 0 else A
+            q.wait_ge(e_u, 1)
+            copy(q, T.dw[:, W * o + PW * k:W * o + PW * k + PW], T.psu[:, 512 * o:512 * o + PW], e_d)
+
+    e_gt = [ev() for _ in range(2)]
+    e_gl = [ev() for _ in range(2)]
+    e_gm = [ev() for _ in range(2)]
+    e_t, e_h, e_hq, e_y, e_ye = ([ev() for _ in range(4)] for _ in range(5))
+    e_out = ev()
+    hs = S // 2
+    for q in (V, A):
+        q.wait_ge(e_s16, 1)
+        q.wait_ge(e_sl, 8)
+
+    def pick(o):
+        for h, q in enumerate((V, A)):
+            q.wait_ge(T.sem["dw%d" % o], 4)
+            copy(q, T.gt[:, S * o + hs * h:S * o + hs * h + hs],
+                 T.dw[:, W * o:W * o + W].indirect(T.s16[:, 16 * h:16 * h + 16]), e_gt[o])
+
+    def pick_both():
+        for h, q in enumerate((V, A)):
+            q.wait_ge(T.sem.dw2, 4)
+            q.wait_ge(T.sem.dw3, 4)
+            copy(q, T.gl[:, S * h:S * h + S], T.dw[:, 2 * W:4 * W].indirect(T.sl[:, 32 * h:32 * h + 32]), e_gl[h])
+        for k in range(2):
+            for h in range(2):
+                if k == 0:
+                    Y.wait_ge(e_gl[h], 1)
+                for a in (2 * h, 2 * h + 1):
+                    for s in (2 * k, 2 * k + 1):
+                        Y.dma_start(T.gm[32 * a:32 * a + 32, hs * s:hs * s + hs],
+                                    T.gl[32 * s:32 * s + 32, hs * a:hs * a + hs]).then_inc(e_gm[k], 16)
+
+    def turn(o):
+        P.wait_ge(e_gt[o], 2)
+        b = 512 * o
+        for t in range(4):
+            P.transpose(T.pst[:, b + t:b + 512:4], T.gt[:, b + t:b + 512:4], T.ident[:]).then_inc(e_t[o], 1)
+
+    def turn_here(o):
+        V.wait_ge(e_gm[o - 2], 128)
+        b = S * (o - 2)
+        for t in range(4):
+            V.transpose(T.ht[:, 512 * o + t:512 * o + 512:4], T.gm[:, b + t:b + S:4]).then_inc(e_h[o], 1)
+
+    def empty(o, q):
+        q.wait_ge(e_t[o], 4)
+        copy(q, T.ht[:, 512 * o:512 * o + 512], T.pst[:, 512 * o:512 * o + 512], e_h[o])
+
+    def quant(o):
+        n = 1 if o < 2 else 4
+        V.wait_ge(e_h[o], n)
+        V.quantize_mx(T.hq[:, 128 * o:128 * o + 128], T.hp[:, 128 * o:128 * o + 128],
+                      T.ht[:, 512 * o:512 * o + 512]).then_inc(e_hq[o], 1)
+        Y.wait_ge(e_h[o], n)
+        Y.dma_start(T.h[:, 512 * o:512 * o + 512], T.ht[:, 512 * o:512 * o + 512]).then_inc(e_out, 16)
+
+    bank = {}
+
+    def product(o):
+        n = len(bank)
+        bank[o] = T.psy[:, 512 * n:512 * n + NA] if n < 2 else T.psu[:, 512 * (n - 2):512 * (n - 2) + NA]
+        P.wait_ge(e_hq[o], 1)
+        P.matmul_mx(bank[o], T.hq[:, 128 * o:128 * o + 128], T.hp[:, 128 * o:128 * o + 128], T.aq[:], T.ap[:],
+                    True, True).then_inc(e_y[o], 1)
+
+    def y_out(o, q):
+        q.wait_ge(e_y[o], 1)
+        copy(q, T.yt[:, NA * o:NA * o + NA], bank[o], e_ye[o])
+        Y.wait_ge(e_ye[o], 1)
+        Y.dma_start(T.y[:, NA * o:NA * o + NA], T.yt[:, NA * o:NA * o + NA]).then_inc(e_out, 16)
+
+    P.wait_ge(e_id, 1)
+    P.wait_ge(e_aq, 1)
+    step = {"p": pick, "t": turn, "l": turn_here, "q": quant, "m": product, "e": empty, "y": y_out}
+    for w in TAIL.split():
+        if w == "L":
+            pick_both()
+        elif w[0] in "ey":
+            step[w[0]](int(w[1]), V if w[2:] == "V" else A)
+        else:
+            step[w[0]](int(w[1]))
+    Y.wait_ge(e_out, 128)

@@ -5,38 +5,42 @@ N, CAPP, NV, NA, S = 8, 96, 512, 256, 512
 W = N * CAPP
 LW = CAPP // 16
 COPY = ActivationFunctionType.Copy
-OWNAT = 1.5
-UORD = [0, 3, 2, 1]
-TAIL = "p0 L p1 t0 t1 e0V q0 m0 y0 e1 l2 q2 m2 q1 m1 y2 y1 l3 q3 m3 y3V"
+BATCH = ["10 11", "30 31 01", "20 21"]
+LISTS = [[0], [1, 2]]
+GATHER = ["VAVA", "VAVA", "VAAA"]
+NEAR = 4
+ROAD = "PLLL"
+LATE = "P"
+SELF = [3]
+UNP = "VAVA"
+TAIL = "p1 p0 t0 p2 p3 e0 l1 h1 q1 q0 h0 m1 m0 y1 l2 h2 q2 y0 l3 q3 m2 h3 y2 z3"
+NB = len(BATCH)
+WIDE = [max(128, CAPP * len(b.split())) for b in BATCH] + [128]
+LS = 4 * LW
 
 SCRATCH = {
     "w32": ("sbuf", [128, N * LW], "int32"),
     "w16": ("sbuf", [128, N * LW], "uint16"),
-    "lst": ("sbuf", [128, N * LW], "uint16"),
+    "lst": ("sbuf", [128, LS * NB], "uint16"),
     "s32": ("sbuf", [128, S // 16], "int32"),
     "s16": ("sbuf", [128, S // 16], "uint16"),
-    "sl": ("sbuf", [128, S // 8], "uint16"),
     "vt": ("sbuf", [128, 4 * NV], "bfloat16"),
     "at": ("sbuf", [128, 4 * NA], "bfloat16"),
     "aq": ("sbuf", [128, NA], "float8_e4m3fn_x4"),
     "ap": ("sbuf", [128, NA], "uint8"),
-    "mi": ("sbuf", [128, 128], "float32"),
+    "mP": ("sbuf", [128, 128], "bfloat16"),
+    "mL": ("sbuf", [128, 128], "bfloat16"),
     "pi": ("sbuf", [128, 16], "float32"),
-    "jt": ("sbuf", [128, 512], "bfloat16"),
-    "jl": ("sbuf", [128, 512], "bfloat16"),
     "et": ("sbuf", [128, 2048], "bfloat16"),
     "eq": ("sbuf", [128, 512], "float8_e4m3fn_x4"),
     "ep": ("sbuf", [128, 512], "uint8"),
     "ident": ("sbuf", [128, 128], "float32"),
-    "x0": ("sbuf", [128, 512], "bfloat16"),
-    "q0": ("sbuf", [128, 128], "float8_e4m3fn_x4"),
-    "p0": ("sbuf", [128, 128], "uint8"),
     "cq": ("sbuf", [128, W], "float8_e4m3fn_x4"),
     "cp": ("sbuf", [128, W], "uint8"),
     "dw": ("sbuf", [128, 4 * W], "bfloat16"),
-    "gt": ("sbuf", [128, 2 * S], "float32"),
-    "gl": ("sbuf", [128, 2 * S], "bfloat16"),
-    "gm": ("sbuf", [128, 2 * S], "bfloat16"),
+    "gt": ("sbuf", [128, 4 * S], "float32"),
+    "gl": ("sbuf", [128, 4 * S], "bfloat16"),
+    "gm": ("sbuf", [128, 4 * S], "bfloat16"),
     "ht": ("sbuf", [128, 4 * S], "bfloat16"),
     "hq": ("sbuf", [128, S], "float8_e4m3fn_x4"),
     "hp": ("sbuf", [128, S], "uint8"),
@@ -45,46 +49,49 @@ SCRATCH = {
     "pst": ("psum", [128, 1024], "float32"),
     "psy": ("psum", [128, 1024], "float32"),
 }
-for _k, _n in ((1, 2), (2, 3), (3, 2)):
-    SCRATCH["x%d" % _k] = ("sbuf", [128, 4 * CAPP * _n], "bfloat16")
-    SCRATCH["q%d" % _k] = ("sbuf", [128, CAPP * _n], "float8_e4m3fn_x4")
-    SCRATCH["p%d" % _k] = ("sbuf", [128, CAPP * _n], "uint8")
-NEV = 96
-SEMAPHORES = (["lst1", "lst2", "lst3", "loc"] + ["arr%d" % k for k in range(N // 2)] + ["dw%d" % k for k in range(4)]
-              + ["e%d" % k for k in range(NEV)])
+for _i, _n in enumerate(WIDE):
+    SCRATCH["x%d" % _i] = ("sbuf", [128, 4 * _n], "bfloat16")
+    SCRATCH["q%d" % _i] = ("sbuf", [128, _n], "float8_e4m3fn_x4")
+    SCRATCH["p%d" % _i] = ("sbuf", [128, _n], "uint8")
+NEV = 120
+SEMAPHORES = (["loc", "left", "near"] + ["lst%d" % i for i in range(NB)] + ["arr%d" % i for i in range(NB)]
+              + ["bank%d" % k for k in range(4)] + ["e%d" % k for k in range(NEV)])
 
 
-def relation(topo, a, b):
-    ca, cb = topo.chip(a), topo.chip(b)
-    return 2 if ca == cb else 1 if topo.same_plane(ca, cb) else 0
+def batches(r):
+    return [[2 * ((r // 2 + int(w[0])) % (N // 2)) + (r + int(w[1])) % 2 for w in b.split()] for b in BATCH]
 
 
-def batches(topo, cores, r):
-    rel = [relation(topo, cores[r], c) for c in cores]
-    near = sorted([q for q in range(N) if q != r], key=lambda q: (q // 2 - r // 2) % (N // 2) * N + q)
-    far = [q for q in near if rel[q] == 0]
-    return [far[:2], far[2:] + [q for q in near if rel[q] == 2], [q for q in near if rel[q] == 1]]
+def served(r, i):
+    return [q for q in range(N) if q != r and r in batches(q)[i]]
 
 
-def peers(topo, cores, r):
-    return [q for b in batches(topo, cores, r) for q in b]
+def asked(r, call):
+    return [q for i in call for q in served(r, i)]
 
 
 def lanes(topo, cores, r, group):
-    off = [q for q in group if relation(topo, cores[r], cores[q]) < 2]
-    eng = topo.engines(cores[r], cores[off[0]])
-    wide = 1
-    while 2 * wide * len(off) <= len(eng):
-        wide *= 2
-    spare = (len(eng) - wide * len(off)) // wide
-    out, at = {}, 0
-    for k, q in enumerate(off):
-        n = 2 * wide if len(off) - k <= spare else wide
-        out[q] = eng[at:at + n]
-        at += n
+    off = [q for q in group if topo.chip(cores[r]) != topo.chip(cores[q])]
+    eng = topo.engines(cores[r], cores[(r + 2) % N])
+    wide = len(eng) // max(1, len(off))
+    out = {q: eng[wide * k:wide * k + wide] for k, q in enumerate(off)}
     for q in group:
         if q not in out:
-            out[q] = [e for e in topo.engines(cores[r], cores[q]) if e not in eng][:2]
+            out[q] = [e for e in topo.engines(cores[r], cores[q]) if e not in eng][:NEAR]
+    return out
+
+
+def runs(r):
+    have, done, out = {r}, set(), []
+    for i in range(NB):
+        have |= set(served(r, i))
+        run = []
+        for k in range(N // 2):
+            new = [q for q in (2 * k, 2 * k + 1) if q not in done]
+            if new and {2 * k, 2 * k + 1} <= have:
+                run.append((2 * CAPP * k, CAPP * new[0], CAPP * new[-1] + CAPP))
+                done |= set(new)
+        out.append(run)
     return out
 
 
@@ -94,8 +101,7 @@ def rank_program(g, core, T, topo):
         return
     cores = list(T.cores)
     V, A, P, Y = g.vector, g.scalar, g.tensor, g.sync
-    order = peers(topo, cores, r)
-    used, nloc = [0], [0]
+    used, nloc = [0], {"loc": 0, "left": 0}
 
     def ev():
         used[0] += 1
@@ -107,7 +113,7 @@ def rank_program(g, core, T, topo):
         else:
             A.activation(out, src, COPY).then_inc(sem, 1)
 
-    def send(group, piece, sem_of):
+    def send(group, piece, sem, gone, near=None):
         eng = lanes(topo, cores, r, group)
         tr = []
         for q in group:
@@ -116,13 +122,10 @@ def rank_program(g, core, T, topo):
             m = 0
             for e in eng[q]:
                 m += 1 << e
-            tr.append(RemoteDMATransfer(dst_ids=[DstId(rid=rid, pnc=pid)], dma_engine_mask=m, remote_sem=sem_of(q),
-                                        src=src, dst=dst))
-            nloc[0] += len(eng[q])
-        g.remote_dma_fused(tr, local_sem=T.sem.loc)
-
-    def batch_of(s, q):
-        return [q in b for b in batches(topo, cores, s)].index(True)
+            tr.append(RemoteDMATransfer(dst_ids=[DstId(rid=rid, pnc=pid)], dma_engine_mask=m, src=src, dst=dst,
+                                        remote_sem=near if near is not None and q // 2 == r // 2 else sem))
+            nloc[gone] += len(eng[q])
+        g.remote_dma_fused(tr, local_sem=T.sem[gone])
 
     e_w, e_v, e_s, e_a = ev(), ev(), ev(), ev()
     for k in range(8):
@@ -132,64 +135,83 @@ def rank_program(g, core, T, topo):
         Y.dma_start(T.s32[16 * k:16 * k + 16, :], T.slot[:]).then_inc(e_s, 16)
     Y.dma_start(T.at[:], T.a[:]).then_inc(e_a, 16)
 
-    e_i, e_z, e_j, e_k = ev(), ev(), ev(), ev()
-    g.iota(T.mi[:], [[1, 128]], 0, 0, allow_small_or_imprecise_dtypes=True).then_inc(e_i, 1)
-    g.iota(T.pi[:], [[-32, 16]], 0, 4, allow_small_or_imprecise_dtypes=True).then_inc(e_i, 1)
-    V.memset(T.x0[:, 4 * CAPP:512], 0.0).then_inc(e_z, 1)
-    V.wait_ge(e_i, 2)
-    for t in range(4):
-        V.tensor_scalar(T.jt[:, t:512:4], T.mi[:], float(t), None, AluOpType.subtract).then_inc(e_j, 1)
+    e_z, e_c = ev(), ev()
+    e_i, e_eq = {road: ev() for road in "PL"}, {road: ev() for road in "PL"}
 
-    e_c = ev()
+    def rows(road):
+        g.iota(T["m" + road][:], {"P": [[1, 128]], "L": [[1, 32], [32, 4]]}[road], 0, 0,
+               allow_small_or_imprecise_dtypes=True).then_inc(e_i[road], 1)
+
+    def onehot(road):
+        e_e, mine = ev(), [o for o in range(4) if ROAD[o] == road]
+        V.wait_ge(e_pi, 1)
+        V.wait_ge(e_i[road], 1)
+        for o in mine:
+            for t in range(4):
+                V.tensor_scalar(T.et[:, 512 * o + t:512 * o + 512:4], T["m" + road][:], T.pi[:, 4 * o + t:4 * o + t + 1], None,
+                                AluOpType.is_equal).then_inc(e_e, 1)
+        V.wait_ge(e_e, 4 * len(mine))
+        for o in mine:
+            if o == 0 or ROAD[o - 1] != road:
+                n = len(ROAD[o:]) - len(ROAD[o:].lstrip(road))
+                V.quantize_mx(T.eq[:, 128 * o:128 * (o + n)], T.ep[:, 128 * o:128 * (o + n)],
+                              T.et[:, 512 * o:512 * (o + n)]).then_inc(e_eq[road], n)
+
+    e_pi = ev()
+    g.iota(T.pi[:], [[-128, 4], [1, 4]], 0, 4, allow_small_or_imprecise_dtypes=True).then_inc(e_pi, 1)
+    early = [road for road in sorted(set(ROAD)) if road not in LATE]
+    late = [road for road in sorted(set(ROAD)) if road in LATE]
+    for road in early:
+        rows(road)
+    nz = 0
+    for i, n in enumerate([CAPP * len(grp) for grp in batches(r)] + [CAPP]):
+        if n < 128:
+            V.memset(T["x%d" % i][:, 4 * n:512], 0.0).then_inc(e_z, 1)
+            nz += 1
+
     V.wait_ge(e_w, 128)
     V.tensor_scalar(T.w16[:], T.w32[:], 0.0, 4.0, AluOpType.max, AluOpType.mult).then_inc(e_c, 1)
+    g.wait_ge(e_c, 1)
 
     def list_piece(q):
-        k = peers(topo, cores, q).index(r)
-        return T.w16[:, LW * q:LW * q + LW], T.lst[:, LW * k:LW * k + LW]
+        i = [r in b for b in batches(q)].index(True)
+        k = LS * i + LW * batches(q)[i].index(r)
+        return T.w16[:, LW * q:LW * q + LW], T.lst[:, k:k + LW]
 
-    g.wait_ge(e_c, 1)
-    send(order, list_piece, lambda q: T.sem["lst%d" % (1 + batch_of(q, r))])
+    for call in LISTS:
+        send(asked(r, call), list_piece, T.sem["lst%d" % call[0]], "left")
+    for road in late:
+        rows(road)
+    for road in early:
+        onehot(road)
 
-    e_e, e_eq = ev(), ev()
-    V.wait_ge(e_j, 4)
-    for s in range(4):
-        V.tensor_scalar(T.jl[:, 128 * s:128 * s + 128], T.jt[:, 128 * s:128 * s + 128], 32.0 * s, None,
-                        AluOpType.add).then_inc(e_k, 1)
-    for o in range(2):
-        V.tensor_scalar(T.et[:, 512 * o:512 * o + 512], T.jt[:], T.pi[:, 4 * o:4 * o + 1], None,
-                        AluOpType.is_equal).then_inc(e_e, 1)
-    V.wait_ge(e_k, 4)
-    for b in range(2):
-        V.tensor_scalar(T.et[:, 1024 + 512 * b:1536 + 512 * b], T.jl[:], T.pi[:, 8 + b:9 + b], None,
-                        AluOpType.is_equal).then_inc(e_e, 1)
-    V.wait_ge(e_e, 4)
-    V.quantize_mx(T.eq[:], T.ep[:], T.et[:]).then_inc(e_eq, 1)
-
-    e_g0, e_q0, e_own = ev(), ev(), ev()
-    A.wait_ge(e_v, 16)
+    e_g, e_q, e_own = ev(), ev(), ev()
+    x, qb, pb = (T["%s%d" % (c, NB)] for c in "xqp")
     A.wait_ge(e_c, 1)
+    A.wait_ge(e_v, 16)
     for t in range(4):
-        A.activation(T.x0[:, t:4 * CAPP:4], T.vt[:, t:4 * NV].indirect(T.w16[:, LW * r:LW * r + LW]), COPY).then_inc(e_g0, 1)
-    V.wait_ge(e_z, 1)
-    V.wait_ge(e_g0, 4)
-    V.quantize_mx(T.q0[:], T.p0[:], T.x0[:]).then_inc(e_q0, 1)
-    Y.wait_ge(e_q0, 1)
-    Y.dma_start(T.cq[:, CAPP * r:CAPP * r + CAPP].bitcast(dt.uint8), T.q0[:, 0:CAPP].bitcast(dt.uint8)).then_inc(e_own, 16)
-    Y.dma_start(T.cp[:, CAPP * r:CAPP * r + CAPP], T.p0[:, 0:CAPP]).then_inc(e_own, 16)
+        A.activation(x[:, t:4 * CAPP:4], T.vt[:, t:4 * NV].indirect(T.w16[:, LW * r:LW * r + LW]), COPY).then_inc(e_g, 1)
+    V.wait_ge(e_z, nz)
+    V.wait_ge(e_g, 4)
+    V.quantize_mx(qb[:], pb[:], x[:]).then_inc(e_q, 1)
+    Y.wait_ge(T.sem.left, nloc["left"])
+    Y.wait_ge(e_q, 1)
+    Y.dma_start(T.cq[:, CAPP * r:CAPP * r + CAPP].bitcast(dt.uint8), qb[:, 0:CAPP].bitcast(dt.uint8)).then_inc(e_own, 16)
+    Y.dma_start(T.cp[:, CAPP * r:CAPP * r + CAPP], pb[:, 0:CAPP]).then_inc(e_own, 16)
 
     V.wait_ge(e_v, 16)
-    c0 = 0
-    for i, grp in enumerate(batches(topo, cores, r)):
-        x, qb, pb = T["x%d" % (i + 1)], T["q%d" % (i + 1)], T["p%d" % (i + 1)]
-        need = sum(len(lanes(topo, cores, s, peers(topo, cores, s))[r]) for s in grp)
+    for i, grp in enumerate(batches(r)):
+        x, qb, pb = (T["%s%d" % (c, i)] for c in "xqp")
         n = CAPP * len(grp)
-        off = T.lst[:, LW * c0:LW * (c0 + len(grp))]
+        off = T.lst[:, LS * i:LS * i + LW * len(grp)]
         e_g, e_q = ev(), ev()
-        V.wait_ge(T.sem["lst%d" % (i + 1)], need)
-        A.wait_ge(T.sem["lst%d" % (i + 1)], need)
+        for call in LISTS:
+            if call[0] == i:
+                need = sum(len(lanes(topo, cores, q, asked(q, call))[r]) for k in call for q in batches(r)[k])
+                V.wait_ge(T.sem["lst%d" % i], need)
+                A.wait_ge(T.sem["lst%d" % i], need)
         for t in range(4):
-            copy(V if t % 2 == 0 else A, x[:, t:4 * n:4], T.vt[:, t:4 * NV].indirect(off), e_g)
+            copy(V if GATHER[i][t] == "V" else A, x[:, t:4 * n:4], T.vt[:, t:4 * NV].indirect(off), e_g)
         V.wait_ge(e_g, 4)
         V.quantize_mx(qb[:], pb[:], x[:]).then_inc(e_q, 1)
         g.wait_ge(e_q, 1)
@@ -202,120 +224,128 @@ def rank_program(g, core, T, topo):
             k = CAPP * grp.index(q)
             return pb[:, k:k + CAPP], T.cp[:, CAPP * r:CAPP * r + CAPP]
 
-        send(grp, codes, lambda q: T.sem["arr%d" % (r // 2)])
-        send(grp, planes, lambda q: T.sem["arr%d" % (r // 2)])
-        c0 += len(grp)
-    g.wait_ge(T.sem.loc, nloc[0])
+        send(grp, codes, T.sem["arr%d" % i], "loc", T.sem.near)
+        send(grp, planes, T.sem["arr%d" % i], "loc", T.sem.near)
+    g.wait_ge(T.sem.loc, nloc["loc"])
 
-    e_id, e_s16, e_sl, e_aq = ev(), ev(), ev(), ev()
-    V.tensor_scalar(T.ident[:], T.mi[:], 4.0, T.pi[:, 0:1], AluOpType.mult, AluOpType.is_equal).then_inc(e_id, 1)
+    e_s16, e_id, e_aq = ev(), ev(), ev()
+    for road in late:
+        onehot(road)
     V.wait_ge(e_s, 128)
     V.tensor_copy(T.s16[:], T.s32[:]).then_inc(e_s16, 1)
-    for a in range(4):
-        for b in range(2):
-            V.tensor_scalar(T.sl[:, 16 * a + 8 * b:16 * a + 8 * b + 8], T.s32[:, 8 * a:8 * a + 8], float(b * W), None,
-                            AluOpType.add).then_inc(e_sl, 1)
+    if "P" in ROAD:
+        V.tensor_scalar(T.ident[:], T.mP[:], 4.0, T.pi[:, 0:1], AluOpType.mult, AluOpType.is_equal).then_inc(e_id, 1)
     V.wait_ge(e_a, 16)
     V.quantize_mx(T.aq[:], T.ap[:], T.at[:]).then_inc(e_aq, 1)
 
-    PW = 2 * CAPP
-    pairs = sorted(range(N // 2), key=lambda k: OWNAT if k == r // 2 else batch_of(2 * k, r))
-    P.wait_ge(e_eq, 1)
-    for c, k in enumerate(pairs):
-        need = 0
-        for s in (2 * k, 2 * k + 1):
-            if s != r:
-                need += 2 * len(lanes(topo, cores, s, batches(topo, cores, s)[batch_of(s, r)])[r])
-        if k == r // 2:
-            P.wait_ge(e_own, 32)
-        P.wait_ge(T.sem["arr%d" % k], need)
-        for o in UORD:
-            e_u, e_d = ev(), T.sem["dw%d" % o]
-            if c:
-                P.wait_ge(e_d, c)
-            P.matmul_mx(T.psu[:, 512 * o:512 * o + PW], T.eq[:, 128 * o:128 * o + 128], T.ep[:, 128 * o:128 * o + 128],
-                        T.cq[:, PW * k:PW * k + PW], T.cp[:, PW * k:PW * k + PW], True, True).then_inc(e_u, 1)
-            q = V if o % 2 == 0 else A
-            q.wait_ge(e_u, 1)
-            copy(q, T.dw[:, W * o + PW * k:W * o + PW * k + PW], T.psu[:, 512 * o:512 * o + PW], e_d)
+    freed = 0
+    for road in set(ROAD):
+        P.wait_ge(e_eq[road], ROAD.count(road))
+    for i, run in enumerate(runs(r)):
+        far = False
+        for first, lo, hi in sorted(run, key=lambda c: c[0] != 2 * CAPP * (r // 2)):
+            if first == 2 * CAPP * (r // 2):
+                P.wait_ge(e_own, 32)
+                P.wait_ge(T.sem.near, 2 * NEAR)
+            elif not far:
+                far = True
+                P.wait_ge(T.sem["arr%d" % i], sum(2 * len(lanes(topo, cores, q, batches(q)[i])[r]) for q in served(r, i)
+                                                  if q // 2 != r // 2))
+            end = first + 2 * CAPP
+            for o in range(4):
+                e_u, e_d = ev(), T.sem["bank%d" % o]
+                if freed:
+                    P.wait_ge(e_d, freed)
+                P.matmul_mx(T.psu[:, 512 * o:512 * o + end - first], T.eq[:, 128 * o:128 * o + 128],
+                            T.ep[:, 128 * o:128 * o + 128], T.cq[:, first:end], T.cp[:, first:end], True, True).then_inc(e_u, 1)
+                q = V if UNP[o] == "V" else A
+                q.wait_ge(e_u, 1)
+                copy(q, T.dw[:, W * o + lo:W * o + hi], T.psu[:, 512 * o + lo - first:512 * o + hi - first], e_d)
+            freed += 1
 
-    e_gt = [ev() for _ in range(2)]
-    e_gl = [ev() for _ in range(2)]
-    e_gm = [ev() for _ in range(2)]
-    e_t, e_h, e_hq, e_y, e_ye = ([ev() for _ in range(4)] for _ in range(5))
+    e_p, e_fv, e_fa, e_t, e_h, e_hq, e_y, e_ye = ([ev() for _ in range(4)] for _ in range(8))
     e_out = ev()
+    nout = [0]
     hs = S // 2
-    for q in (V, A):
-        q.wait_ge(e_s16, 1)
-        q.wait_ge(e_sl, 8)
+
+    def store(q, out, src):
+        q.dma_start(out, src).then_inc(e_out, 16)
+        nout[0] += 16
 
     def pick(o):
-        for h, q in enumerate((V, A)):
-            q.wait_ge(T.sem["dw%d" % o], 4)
-            copy(q, T.gt[:, S * o + hs * h:S * o + hs * h + hs],
-                 T.dw[:, W * o:W * o + W].indirect(T.s16[:, 16 * h:16 * h + 16]), e_gt[o])
-
-    def pick_both():
-        for h, q in enumerate((V, A)):
-            q.wait_ge(T.sem.dw2, 4)
-            q.wait_ge(T.sem.dw3, 4)
-            copy(q, T.gl[:, S * h:S * h + S], T.dw[:, 2 * W:4 * W].indirect(T.sl[:, 32 * h:32 * h + 32]), e_gl[h])
-        for k in range(2):
-            for h in range(2):
-                if k == 0:
-                    Y.wait_ge(e_gl[h], 1)
-                for a in (2 * h, 2 * h + 1):
-                    for s in (2 * k, 2 * k + 1):
-                        Y.dma_start(T.gm[32 * a:32 * a + 32, hs * s:hs * s + hs],
-                                    T.gl[32 * s:32 * s + 32, hs * a:hs * a + hs]).then_inc(e_gm[k], 16)
+        to = T.gt if ROAD[o] == "P" else T.gl
+        for h, q, e in ((0, V, e_fv[o]), (1, A, e_fa[o])):
+            q.wait_ge(T.sem["bank%d" % o], freed)
+            copy(q, to[:, S * o + hs * h:S * o + hs * h + hs], T.dw[:, W * o:W * o + W].indirect(T.s16[:, 16 * h:16 * h + 16]), e)
+        for a in range(4 * (ROAD[o] == "L")):
+            q = A if a == 3 and o in SELF else Y
+            if a % 2 == 0 or q is A:
+                q.wait_ge((e_fv, e_fa)[a // 2][o], 1)
+            q.dma_start(T.gm[32 * a:32 * a + 32, S * o:S * o + S],
+                        to[:, S * o + 128 * a:S * o + 128 * a + 128]).then_inc(e_p[o], 16)
 
     def turn(o):
-        P.wait_ge(e_gt[o], 2)
-        b = 512 * o
+        P.wait_ge(e_fv[o], 1)
+        P.wait_ge(e_fa[o], 1)
+        b = 512 * ROAD[:o].count("P")
         for t in range(4):
-            P.transpose(T.pst[:, b + t:b + 512:4], T.gt[:, b + t:b + 512:4], T.ident[:]).then_inc(e_t[o], 1)
+            P.transpose(T.pst[:, b + t:b + 512:4], T.gt[:, S * o + t:S * o + S:4], T.ident[:]).then_inc(e_t[o], 1)
 
     def turn_here(o):
-        V.wait_ge(e_gm[o - 2], 128)
-        b = S * (o - 2)
+        V.wait_ge(e_p[o], 64)
         for t in range(4):
-            V.transpose(T.ht[:, 512 * o + t:512 * o + 512:4], T.gm[:, b + t:b + S:4]).then_inc(e_h[o], 1)
+            V.transpose(T.ht[:, 512 * o + t:512 * o + 512:4], T.gm[:, S * o + t:S * o + S:4]).then_inc(e_h[o], 1)
 
     def empty(o, q):
         q.wait_ge(e_t[o], 4)
-        copy(q, T.ht[:, 512 * o:512 * o + 512], T.pst[:, 512 * o:512 * o + 512], e_h[o])
+        b = 512 * ROAD[:o].count("P")
+        copy(q, T.ht[:, 512 * o:512 * o + 512], T.pst[:, b:b + 512], e_h[o])
 
     def quant(o):
-        n = 1 if o < 2 else 4
-        V.wait_ge(e_h[o], n)
+        V.wait_ge(e_h[o], 1 if ROAD[o] == "P" else 4)
         V.quantize_mx(T.hq[:, 128 * o:128 * o + 128], T.hp[:, 128 * o:128 * o + 128],
                       T.ht[:, 512 * o:512 * o + 512]).then_inc(e_hq[o], 1)
-        Y.wait_ge(e_h[o], n)
-        Y.dma_start(T.h[:, 512 * o:512 * o + 512], T.ht[:, 512 * o:512 * o + 512]).then_inc(e_out, 16)
 
+    def h_out(o):
+        Y.wait_ge(e_h[o], 1 if ROAD[o] == "P" else 4)
+        store(Y, T.h[:, 512 * o:512 * o + 512], T.ht[:, 512 * o:512 * o + 512])
+
+    banks = [T.psy[:, 0:NA], T.psy[:, 512:512 + NA], T.psu[:, 0:NA]]
     bank = {}
 
     def product(o):
-        n = len(bank)
-        bank[o] = T.psy[:, 512 * n:512 * n + NA] if n < 2 else T.psu[:, 512 * (n - 2):512 * (n - 2) + NA]
+        bank[o] = banks[len(bank)] if len(bank) < 3 else T.psu[:, 512:512 + NA]
         P.wait_ge(e_hq[o], 1)
-        P.matmul_mx(bank[o], T.hq[:, 128 * o:128 * o + 128], T.hp[:, 128 * o:128 * o + 128], T.aq[:], T.ap[:],
-                    True, True).then_inc(e_y[o], 1)
+        P.matmul_mx(bank[o], T.hq[:, 128 * o:128 * o + 128], T.hp[:, 128 * o:128 * o + 128],
+                    T.aq[:], T.ap[:], True, True).then_inc(e_y[o], 1)
 
     def y_out(o, q):
         q.wait_ge(e_y[o], 1)
         copy(q, T.yt[:, NA * o:NA * o + NA], bank[o], e_ye[o])
         Y.wait_ge(e_ye[o], 1)
-        Y.dma_start(T.y[:, NA * o:NA * o + NA], T.yt[:, NA * o:NA * o + NA]).then_inc(e_out, 16)
+        store(Y, T.y[:, NA * o:NA * o + NA], T.yt[:, NA * o:NA * o + NA])
 
-    P.wait_ge(e_id, 1)
+    def last(o):
+        P.wait_ge(e_hq[o], 1)
+        for h, q, d in ((0, V, Y), (1, A, A)):
+            e_m, e_o = ev(), ev()
+            b, c = T.psu[:, 512 * (h + 1):512 * (h + 1) + 128], NA * o + 128 * h
+            P.matmul_mx(b, T.hq[:, 128 * o:128 * o + 128], T.hp[:, 128 * o:128 * o + 128],
+                        T.aq[:, 128 * h:128 * h + 128], T.ap[:, 128 * h:128 * h + 128], True, True).then_inc(e_m, 1)
+            q.wait_ge(e_m, 1)
+            copy(q, T.yt[:, c:c + 128], b, e_o)
+            d.wait_ge(e_o, 1)
+            store(d, T.y[:, c:c + 128], T.yt[:, c:c + 128])
+
+    if "P" in ROAD:
+        P.wait_ge(e_id, 1)
     P.wait_ge(e_aq, 1)
-    step = {"p": pick, "t": turn, "l": turn_here, "q": quant, "m": product, "e": empty, "y": y_out}
+    A.wait_ge(e_s16, 1)
+    V.wait_ge(e_s16, 1)
+    step = {"p": pick, "t": turn, "l": turn_here, "q": quant, "m": product, "e": empty, "y": y_out, "h": h_out, "z": last}
     for w in TAIL.split():
-        if w == "L":
-            pick_both()
-        elif w[0] in "ey":
+        if w[0] in "ey":
             step[w[0]](int(w[1]), V if w[2:] == "V" else A)
         else:
             step[w[0]](int(w[1]))
-    Y.wait_ge(e_out, 128)
+    Y.wait_ge(e_out, nout[0])

@@ -5,17 +5,33 @@ N, CAPP, NV, NA, S = 8, 96, 512, 256, 512
 W = N * CAPP
 LW = CAPP // 16
 COPY = ActivationFunctionType.Copy
-BATCH = ["10 11", "30 31 01", "20 21"]
-LISTS = [[0], [1, 2]]
-GATHER = ["VAVA", "VAVA", "VAAA"]
+BATCH = ["p0", "f0 f1", "g0 g1 n1", "p1"]
+CALLS = [["c p0", "s p0"], ["c f0 f1", "s f0 f1"], ["c g0 g1 n1", "s g0 g1 n1"], ["c p1", "s p1"]]
+VIA = ""
+HAND = 8
+MOST = 8
+RUNS = ["n0 p0", "f0 f1", "n1", "g0 g1", "p1"]
+LISTS = ["p0", "f0 f1", "g0 g1 n1", "p1"]
+GATHER = ["VAVA", "VAVA", "VAVA", "VAAA"]
 NEAR = 4
 ROAD = "PLLL"
+UORD = [1, 2, 0, 3]
+EARLY = 0
+GSEL = 3
+WHOLE = 1
+OWNQ = 0
 LATE = "P"
-SELF = [3]
+HALF = 1
+TWO = 1
+OWN = "AAAA"
+SPLIT = [16, 16, 16, 16]
+QUART = [1, 3]
+SELF = [33]
 UNP = "VAVA"
-TAIL = "p1 p0 t0 p2 p3 e0 l1 h1 q1 q0 h0 m1 m0 y1 l2 h2 q2 y0 l3 q3 m2 h3 y2 z3"
+TAIL = "c1V c2 p1 c0V c3 p2 p0 t0 p3 e0 H0 l1 h1 q1 m1 l2 h2 q2 q0 m2 y1 m0 y2 l3 q3 h3 y0 z3"
 NB = len(BATCH)
-WIDE = [max(128, CAPP * len(b.split())) for b in BATCH] + [128]
+GROUPS = [words for b in BATCH for words in b.split("|")]
+WIDE = [max(128, CAPP * len(b.replace("|", " ").split())) for b in BATCH] + [128]
 LS = 4 * LW
 
 SCRATCH = {
@@ -30,6 +46,9 @@ SCRATCH = {
     "ap": ("sbuf", [128, NA], "uint8"),
     "mP": ("sbuf", [128, 128], "bfloat16"),
     "mL": ("sbuf", [128, 128], "bfloat16"),
+    "jL": ("sbuf", [128, 512], "bfloat16"),
+    "ones": ("sbuf", [128, 512], "bfloat16"),
+    "onef": ("sbuf", [128, 128], "float32"),
     "pi": ("sbuf", [128, 16], "float32"),
     "et": ("sbuf", [128, 2048], "bfloat16"),
     "eq": ("sbuf", [128, 512], "float8_e4m3fn_x4"),
@@ -53,53 +72,97 @@ for _i, _n in enumerate(WIDE):
     SCRATCH["x%d" % _i] = ("sbuf", [128, 4 * _n], "bfloat16")
     SCRATCH["q%d" % _i] = ("sbuf", [128, _n], "float8_e4m3fn_x4")
     SCRATCH["p%d" % _i] = ("sbuf", [128, _n], "uint8")
-NEV = 120
-SEMAPHORES = (["loc", "left", "near"] + ["lst%d" % i for i in range(NB)] + ["arr%d" % i for i in range(NB)]
-              + ["bank%d" % k for k in range(4)] + ["e%d" % k for k in range(NEV)])
+NEV = 124
+SEMAPHORES = (["loc", "left", "via0", "via1"] + ["lst%d" % i for i in range(len(GROUPS))] + ["arr%d" % i for i in range(len(RUNS))]
+              + ["bank%d" % k for k in range(8)] + ["e%d" % k for k in range(NEV)])
+
+
+KIN = {}
+
+
+def learn(topo, cores):
+    for r in range(N):
+        far = []
+        for k in range(N // 2):
+            pair = (r // 2 + k) % (N // 2)
+            a, b = topo.chip(cores[r]), topo.chip(cores[2 * pair])
+            if a == b:
+                KIN[r, "n"] = pair
+            elif topo.same_plane(a, b):
+                KIN[r, "p"] = pair
+            else:
+                far.append(pair)
+        KIN[r, "f"], KIN[r, "g"] = far
+
+
+def named(r, words):
+    return [2 * KIN[r, w[0]] + (r + int(w[1])) % 2 for w in words.split()]
 
 
 def batches(r):
-    return [[2 * ((r // 2 + int(w[0])) % (N // 2)) + (r + int(w[1])) % 2 for w in b.split()] for b in BATCH]
+    return [named(r, b.replace("|", " ")) for b in BATCH]
 
 
-def served(r, i):
-    return [q for q in range(N) if q != r and r in batches(q)[i]]
+def asked(r, words):
+    return [q for w in words.split() for q in range(N) if named(q, w) == [r]]
 
 
-def asked(r, call):
-    return [q for i in call for q in served(r, i)]
-
-
-def lanes(topo, cores, r, group):
-    off = [q for q in group if topo.chip(cores[r]) != topo.chip(cores[q])]
+def lanes(topo, cores, r, group, most=16, via=()):
+    off = [q for q in group if topo.chip(cores[r]) != topo.chip(cores[q]) and q not in via]
     eng = topo.engines(cores[r], cores[(r + 2) % N])
-    wide = len(eng) // max(1, len(off))
-    out = {q: eng[wide * k:wide * k + wide] for k, q in enumerate(off)}
-    for q in group:
-        if q not in out:
-            out[q] = [e for e in topo.engines(cores[r], cores[q]) if e not in eng][:NEAR]
+    wide = [1] * len(off)
+    k = 0
+    while off and sum(wide) + wide[k] <= len(eng) and wide[k] < most:
+        wide[k] *= 2
+        k = (k + 1) % len(off)
+    out = {q: eng[sum(wide[:k]):sum(wide[:k + 1])] for k, q in enumerate(off)}
+    rest = [e for e in topo.engines(cores[r], cores[named(r, "n1")[0]]) if e not in eng]
+    for k, q in enumerate([q for q in group if q not in out]):
+        out[q] = rest[NEAR * k:NEAR * k + NEAR]
     return out
+
+
+def helper(topo, cores, r):
+    can = [c for c in topo.cores_of(cores[r]) if topo.die(c) != topo.die(cores[r])
+           and all(topo.may_write(c, cores[q]) for s in (r - r % 2, r - r % 2 + 1) for q in named(s, VIA))]
+    return can[len(can) // 2 * (r % 2)]
+
+
+def hand_on(g, core, T, topo, cores, r):
+    sent = 0
+    for k, q in enumerate(named(r, VIA)):
+        at, eng = place(r, q), topo.engines(core, cores[q])[:HAND]
+        rid, pid, _ = topo.addr(cores[q])
+        g.wait_ge(T.sem["via%d" % k], NEAR)
+        g.remote_dma_fused([RemoteDMATransfer(
+            dst_ids=[DstId(rid=rid, pnc=pid)], dma_engine_mask=sum(1 << e for e in eng),
+            src=T.cq[:, CAPP * k:CAPP * k + CAPP].bitcast(dt.uint8), dst=T.cq[:, at:at + CAPP].bitcast(dt.uint8),
+            remote_sem=T.sem["arr%d" % [r in run for run in runs(q)].index(True)])], local_sem=T.sem.loc)
+        sent += len(eng)
+    g.wait_ge(T.sem.loc, sent)
 
 
 def runs(r):
-    have, done, out = {r}, set(), []
-    for i in range(NB):
-        have |= set(served(r, i))
-        run = []
-        for k in range(N // 2):
-            new = [q for q in (2 * k, 2 * k + 1) if q not in done]
-            if new and {2 * k, 2 * k + 1} <= have:
-                run.append((2 * CAPP * k, CAPP * new[0], CAPP * new[-1] + CAPP))
-                done |= set(new)
-        out.append(run)
+    out = []
+    for words in RUNS:
+        run = asked(r, words)
+        out.append(sorted(run, key=lambda q: ([s // 2 for s in run].index(q // 2), q)))
     return out
 
 
+def place(s, r):
+    return CAPP * [q for run in runs(r) for q in run].index(s)
+
+
 def rank_program(g, core, T, topo):
+    cores = list(T.cores)
+    learn(topo, cores)
     r = T.rank_of(core)
     if r is None:
+        for s in range(N):
+            if VIA and core == helper(topo, cores, s):
+                hand_on(g, core, T, topo, cores, s)
         return
-    cores = list(T.cores)
     V, A, P, Y = g.vector, g.scalar, g.tensor, g.sync
     used, nloc = [0], {"loc": 0, "left": 0}
 
@@ -113,22 +176,22 @@ def rank_program(g, core, T, topo):
         else:
             A.activation(out, src, COPY).then_inc(sem, 1)
 
-    def send(group, piece, sem, gone, near=None):
-        eng = lanes(topo, cores, r, group)
+    def send(group, piece, sem, gone, most=16, via=()):
+        eng = lanes(topo, cores, r, group, most, via)
         tr = []
         for q in group:
-            rid, pid, _ = topo.addr(cores[q])
+            rid, pid, _ = topo.addr(helper(topo, cores, r) if q in via else cores[q])
             src, dst = piece(q)
-            m = 0
-            for e in eng[q]:
-                m += 1 << e
-            tr.append(RemoteDMATransfer(dst_ids=[DstId(rid=rid, pnc=pid)], dma_engine_mask=m, src=src, dst=dst,
-                                        remote_sem=near if near is not None and q // 2 == r // 2 else sem))
+            if q in via:
+                k = via.index(q)
+                dst = T.cq[:, CAPP * k:CAPP * k + CAPP].bitcast(dt.uint8)
+            tr.append(RemoteDMATransfer(dst_ids=[DstId(rid=rid, pnc=pid)], dma_engine_mask=sum(1 << e for e in eng[q]), src=src,
+                                        dst=dst, remote_sem=T.sem["via%d" % k] if q in via else sem(q)))
             nloc[gone] += len(eng[q])
         g.remote_dma_fused(tr, local_sem=T.sem[gone])
 
     e_w, e_v, e_s, e_a = ev(), ev(), ev(), ev()
-    for k in range(8):
+    for k in range(4 if HALF else 8):
         (Y if k % 2 == 0 else A).dma_start(T.w32[16 * k:16 * k + 16, :], T.want[:]).then_inc(e_w, 16)
     Y.dma_start(T.vt[:], T.v[:]).then_inc(e_v, 16)
     for k in range(8):
@@ -136,132 +199,223 @@ def rank_program(g, core, T, topo):
     Y.dma_start(T.at[:], T.a[:]).then_inc(e_a, 16)
 
     e_z, e_c = ev(), ev()
-    e_i, e_eq = {road: ev() for road in "PL"}, {road: ev() for road in "PL"}
+    e_i, e_eq, e_id = {road: ev() for road in "PL"}, ev(), ev()
 
     def rows(road):
         g.iota(T["m" + road][:], {"P": [[1, 128]], "L": [[1, 32], [32, 4]]}[road], 0, 0,
                allow_small_or_imprecise_dtypes=True).then_inc(e_i[road], 1)
 
-    def onehot(road):
-        e_e, mine = ev(), [o for o in range(4) if ROAD[o] == road]
+    e_e = [ev() for _ in range(4)]
+
+    def onehot(o):
+        V.wait_ge(e_i[ROAD[o]], 1)
+        if WHOLE and ROAD[o] == "L":
+            V.tensor_scalar(T.et[:, 512 * o:512 * o + 512], T.jL[:], 192.0 - 128 * o, None,
+                            AluOpType.is_equal).then_inc(e_e[o], 4)
+            return
         V.wait_ge(e_pi, 1)
-        V.wait_ge(e_i[road], 1)
-        for o in mine:
-            for t in range(4):
-                V.tensor_scalar(T.et[:, 512 * o + t:512 * o + 512:4], T["m" + road][:], T.pi[:, 4 * o + t:4 * o + t + 1], None,
-                                AluOpType.is_equal).then_inc(e_e, 1)
-        V.wait_ge(e_e, 4 * len(mine))
-        for o in mine:
-            if o == 0 or ROAD[o - 1] != road:
-                n = len(ROAD[o:]) - len(ROAD[o:].lstrip(road))
-                V.quantize_mx(T.eq[:, 128 * o:128 * (o + n)], T.ep[:, 128 * o:128 * (o + n)],
-                              T.et[:, 512 * o:512 * (o + n)]).then_inc(e_eq[road], n)
+        for t in range(4):
+            V.tensor_scalar(T.et[:, 512 * o + t:512 * o + 512:4], T["m" + ROAD[o]][:], T.pi[:, 4 * o + t:4 * o + t + 1],
+                            None, AluOpType.is_equal).then_inc(e_e[o], 1)
+
+    def swapped(o):
+        A.wait_ge(e_e[o - 2], 4)
+        for h in range(2):
+            A.activation(T.et[64 * h:64 * h + 64, 512 * o:512 * o + 512],
+                         T.et[64 - 64 * h:128 - 64 * h, 512 * o - 1024:512 * o - 512], COPY).then_inc(e_e[o], 2)
+
+    def pack(a, b):
+        for o in range(a, b):
+            V.wait_ge(e_e[o], 4)
+        V.quantize_mx(T.eq[:, 128 * a:128 * b], T.ep[:, 128 * a:128 * b], T.et[:, 512 * a:512 * b]).then_inc(e_eq, 1)
 
     e_pi = ev()
-    g.iota(T.pi[:], [[-128, 4], [1, 4]], 0, 4, allow_small_or_imprecise_dtypes=True).then_inc(e_pi, 1)
-    early = [road for road in sorted(set(ROAD)) if road not in LATE]
-    late = [road for road in sorted(set(ROAD)) if road in LATE]
-    for road in early:
-        rows(road)
+    if WHOLE:
+        g.iota(T.jL[:], [[1, 32], [32, 4], [-1, 4]], 192, -4, allow_small_or_imprecise_dtypes=True).then_inc(e_i["L"], 1)
+    else:
+        g.iota(T.pi[:], [[-128, 4], [1, 4]], 0, 4, allow_small_or_imprecise_dtypes=True).then_inc(e_pi, 1)
+        for road in "LP":
+            rows(road)
     nz = 0
     for i, n in enumerate([CAPP * len(grp) for grp in batches(r)] + [CAPP]):
         if n < 128:
             V.memset(T["x%d" % i][:, 4 * n:512], 0.0).then_inc(e_z, 1)
             nz += 1
+    e_one = ev()
+    if GSEL:
+        A.wait_ge(e_i["L"], 1)
+        for s in range(4):
+            A.activation(T.mP[:, 32 * s:32 * s + 32], T.jL[:, 4 * s:512:16], COPY).then_inc(e_i["P"], 1)
+        V.memset(T.onef[:], 1.0).then_inc(e_one, 1)
+    if EARLY:
+        onehot(1)
+        swapped(3)
 
-    V.wait_ge(e_w, 128)
-    V.tensor_scalar(T.w16[:], T.w32[:], 0.0, 4.0, AluOpType.max, AluOpType.mult).then_inc(e_c, 1)
-    g.wait_ge(e_c, 1)
+    V.wait_ge(e_w, 64 if HALF else 128)
+    for h in range(1 + HALF):
+        n = 64 if HALF else 128
+        V.tensor_scalar(T.w16[n * h:n * h + n, :], T.w32[0:n, :], 0.0, 4.0, AluOpType.max, AluOpType.mult).then_inc(e_c, 1)
+    g.wait_ge(e_c, 1 + HALF)
 
     def list_piece(q):
         i = [r in b for b in batches(q)].index(True)
         k = LS * i + LW * batches(q)[i].index(r)
         return T.w16[:, LW * q:LW * q + LW], T.lst[:, k:k + LW]
 
+    def lists(words, gone):
+        send(asked(r, words), list_piece, lambda q: T.sem["lst%d" % [r in named(q, w) for w in GROUPS].index(True)], gone, MOST)
+
     for call in LISTS:
-        send(asked(r, call), list_piece, T.sem["lst%d" % call[0]], "left")
-    for road in late:
-        rows(road)
-    for road in early:
-        onehot(road)
+        lists(call, "left")
+    if WHOLE and not GSEL:
+        g.iota(T.pi[:], [[-128, 4], [1, 4]], 0, 4, allow_small_or_imprecise_dtypes=True).then_inc(e_pi, 1)
+        rows("P")
 
-    e_g, e_q, e_own = ev(), ev(), ev()
-    x, qb, pb = (T["%s%d" % (c, NB)] for c in "xqp")
-    A.wait_ge(e_c, 1)
-    A.wait_ge(e_v, 16)
-    for t in range(4):
-        A.activation(x[:, t:4 * CAPP:4], T.vt[:, t:4 * NV].indirect(T.w16[:, LW * r:LW * r + LW]), COPY).then_inc(e_g, 1)
+    def tile_p():
+        if GSEL:
+            V.wait_ge(e_i["P"], 4)
+            for t in range(4):
+                V.tensor_scalar(T.et[:, t:512:4], T.mP[:], 192.0 + t, None, AluOpType.is_equal).then_inc(e_e[0], 1)
+            return
+        onehot(0)
+        V.tensor_scalar(T.ident[:], T.mP[:], 4.0, T.pi[:, 0:1], AluOpType.mult, AluOpType.is_equal).then_inc(e_id, 1)
+
+    if not EARLY:
+        onehot(1)
+        onehot(3)
+    onehot(2)
+    if not LATE:
+        tile_p()
+    pack(1 if LATE else 0, 4)
+
+    e_own = ev()
+
+    e_og = ev()
+
+    def own():
+        x = T["x%d" % NB]
+        for t in range(4):
+            copy(V if OWN[t] == "V" else A, x[:, t:4 * CAPP:4], T.vt[:, t:4 * NV].indirect(T.w16[:, LW * r:LW * r + LW]), e_og)
+        if not OWNQ:
+            own_codes()
+
+    def own_codes():
+        e_q = ev()
+        x, qb, pb = (T["%s%d" % (c, NB)] for c in "xqp")
+        V.wait_ge(e_og, 4)
+        V.quantize_mx(qb[:], pb[:], x[:]).then_inc(e_q, 1)
+        Y.wait_ge(e_q, 1)
+        at = place(r, r)
+        Y.dma_start(T.cq[:, at:at + CAPP].bitcast(dt.uint8), qb[:, 0:CAPP].bitcast(dt.uint8)).then_inc(e_own, 16)
+        Y.dma_start(T.cp[:, at:at + CAPP], pb[:, 0:CAPP]).then_inc(e_own, 16)
+
+    for q in (V, A):
+        q.wait_ge(e_c, 1 + HALF)
+        q.wait_ge(e_v, 16)
     V.wait_ge(e_z, nz)
-    V.wait_ge(e_g, 4)
-    V.quantize_mx(qb[:], pb[:], x[:]).then_inc(e_q, 1)
     Y.wait_ge(T.sem.left, nloc["left"])
-    Y.wait_ge(e_q, 1)
-    Y.dma_start(T.cq[:, CAPP * r:CAPP * r + CAPP].bitcast(dt.uint8), qb[:, 0:CAPP].bitcast(dt.uint8)).then_inc(e_own, 16)
-    Y.dma_start(T.cp[:, CAPP * r:CAPP * r + CAPP], pb[:, 0:CAPP]).then_inc(e_own, 16)
+    if OWN[4:] == "":
+        own()
 
-    V.wait_ge(e_v, 16)
+    def made(q):
+        i = [q in b for b in batches(r)].index(True)
+        return i, CAPP * batches(r)[i].index(q), place(r, q)
+
+    def codes(q):
+        i, k, at = made(q)
+        return T["q%d" % i][:, k:k + CAPP].bitcast(dt.uint8), T.cq[:, at:at + CAPP].bitcast(dt.uint8)
+
+    def planes(q):
+        i, k, at = made(q)
+        return T["p%d" % i][:, k:k + CAPP], T.cp[:, at:at + CAPP]
+
     for i, grp in enumerate(batches(r)):
         x, qb, pb = (T["%s%d" % (c, i)] for c in "xqp")
-        n = CAPP * len(grp)
-        off = T.lst[:, LS * i:LS * i + LW * len(grp)]
         e_g, e_q = ev(), ev()
-        for call in LISTS:
-            if call[0] == i:
-                need = sum(len(lanes(topo, cores, q, asked(q, call))[r]) for k in call for q in batches(r)[k])
-                V.wait_ge(T.sem["lst%d" % i], need)
-                A.wait_ge(T.sem["lst%d" % i], need)
-        for t in range(4):
-            copy(V if GATHER[i][t] == "V" else A, x[:, t:4 * n:4], T.vt[:, t:4 * NV].indirect(off), e_g)
-        V.wait_ge(e_g, 4)
+        for words in BATCH[i].split("|"):
+            k, part = GROUPS.index(words), named(r, words)
+            lo, hi = grp.index(part[0]), grp.index(part[-1]) + 1
+            need = sum(len(lanes(topo, cores, q, asked(q, call), MOST)[r])
+                       for call in LISTS for q in named(r, call) if q in part)
+            V.wait_ge(T.sem["lst%d" % k], need)
+            A.wait_ge(T.sem["lst%d" % k], need)
+            for t in range(4):
+                copy(V if GATHER[k][t] == "V" else A, x[:, 4 * CAPP * lo + t:4 * CAPP * hi:4],
+                     T.vt[:, t:4 * NV].indirect(T.lst[:, LS * i + LW * lo:LS * i + LW * hi]), e_g)
+        V.wait_ge(e_g, 4 * len(BATCH[i].split("|")))
         V.quantize_mx(qb[:], pb[:], x[:]).then_inc(e_q, 1)
+        if i + 1 == OWNQ:
+            own_codes()
         g.wait_ge(e_q, 1)
-
-        def codes(q):
-            k = CAPP * grp.index(q)
-            return qb[:, k:k + CAPP].bitcast(dt.uint8), T.cq[:, CAPP * r:CAPP * r + CAPP].bitcast(dt.uint8)
-
-        def planes(q):
-            k = CAPP * grp.index(q)
-            return pb[:, k:k + CAPP], T.cp[:, CAPP * r:CAPP * r + CAPP]
-
-        send(grp, codes, T.sem["arr%d" % i], "loc", T.sem.near)
-        send(grp, planes, T.sem["arr%d" % i], "loc", T.sem.near)
+        for call in CALLS[i]:
+            send(named(r, call[2:]), codes if call[0] == "c" else planes,
+                 lambda q: T.sem["arr%d" % [r in run for run in runs(q)].index(True)], "loc", 8,
+                 named(r, VIA) if call[0] == "c" else ())
+        if GSEL and i == GSEL:
+            g.wait_ge(e_one, 1)
+            g.affine_select(T.ident[:], T.onef[:], [[-1, 128]], AluOpType.is_equal, 0.0, 0, 1).then_inc(e_id, 1)
     g.wait_ge(T.sem.loc, nloc["loc"])
 
-    e_s16, e_id, e_aq = ev(), ev(), ev()
-    for road in late:
-        onehot(road)
+    e_s16, e_aq = ev(), ev()
+    if LATE:
+        tile_p()
+        pack(0, 1)
+    if OWN[4:] != "":
+        own()
     V.wait_ge(e_s, 128)
     V.tensor_copy(T.s16[:], T.s32[:]).then_inc(e_s16, 1)
-    if "P" in ROAD:
-        V.tensor_scalar(T.ident[:], T.mP[:], 4.0, T.pi[:, 0:1], AluOpType.mult, AluOpType.is_equal).then_inc(e_id, 1)
-    V.wait_ge(e_a, 16)
-    V.quantize_mx(T.aq[:], T.ap[:], T.at[:]).then_inc(e_aq, 1)
 
-    freed = 0
-    for road in set(ROAD):
-        P.wait_ge(e_eq[road], ROAD.count(road))
+    def quant_a():
+        V.wait_ge(e_a, 16)
+        V.quantize_mx(T.aq[:], T.ap[:], T.at[:]).then_inc(e_aq, 1)
+
+    if "A" not in TAIL:
+        quant_a()
+
+    freed = [0, 0]
+    P.wait_ge(e_eq, 2 if LATE else 1)
+    todo, e_u = [], {}
+
+    def out_of(o, q):
+        q.wait_ge(e_u[o], 1)
+        for piece in pieces:
+            c, d, n = place(piece[0], r) - first, W * o + CAPP * piece[0], CAPP * len(piece)
+            copy(q, T.dw[:, d:d + n], in_bank(4 * side + o, c, c + n), T.sem["bank%d" % (4 * side + o)])
+
+    def in_bank(k, a, b):
+        return (T.psu, T.psu, T.pst, T.psy)[k // 2][:, 512 * (k if k < 4 else k % 2) + a:512 * (k if k < 4 else k % 2) + b]
+
     for i, run in enumerate(runs(r)):
-        far = False
-        for first, lo, hi in sorted(run, key=lambda c: c[0] != 2 * CAPP * (r // 2)):
-            if first == 2 * CAPP * (r // 2):
-                P.wait_ge(e_own, 32)
-                P.wait_ge(T.sem.near, 2 * NEAR)
-            elif not far:
-                far = True
-                P.wait_ge(T.sem["arr%d" % i], sum(2 * len(lanes(topo, cores, q, batches(q)[i])[r]) for q in served(r, i)
-                                                  if q // 2 != r // 2))
-            end = first + 2 * CAPP
-            for o in range(4):
-                e_u, e_d = ev(), T.sem["bank%d" % o]
-                if freed:
-                    P.wait_ge(e_d, freed)
-                P.matmul_mx(T.psu[:, 512 * o:512 * o + end - first], T.eq[:, 128 * o:128 * o + 128],
-                            T.ep[:, 128 * o:128 * o + 128], T.cq[:, first:end], T.cp[:, first:end], True, True).then_inc(e_u, 1)
-                q = V if UNP[o] == "V" else A
-                q.wait_ge(e_u, 1)
-                copy(q, T.dw[:, W * o + lo:W * o + hi], T.psu[:, 512 * o + lo - first:512 * o + hi - first], e_d)
-            freed += 1
+        if r in run:
+            P.wait_ge(e_own, 32)
+        need = 0
+        for q in run:
+            for call in [call for calls in CALLS for call in calls if r in named(q, call[2:])]:
+                via = named(q, VIA) if call[0] == "c" else ()
+                need += HAND if r in via else len(lanes(topo, cores, q, named(q, call[2:]), 8, via)[r])
+        P.wait_ge(T.sem["arr%d" % i], need)
+        todo += run
+        end = place(todo[-1], r) + CAPP
+        if end < 128:
+            continue
+        first = min(place(todo[0], r), end - 128)
+        side = (len(RUNS) - 1 - i) % 2 * TWO
+        pieces = [[q] for q in todo[:1]]
+        for q in todo[1:]:
+            if q == pieces[-1][-1] + 1:
+                pieces[-1].append(q)
+            else:
+                pieces.append([q])
+        for o in UORD:
+            e_u[o] = ev()
+            if freed[side]:
+                P.wait_ge(T.sem["bank%d" % (4 * side + o)], freed[side])
+            P.matmul_mx(in_bank(4 * side + o, 0, end - first), T.eq[:, 128 * o:128 * o + 128],
+                        T.ep[:, 128 * o:128 * o + 128], T.cq[:, first:end], T.cp[:, first:end], True, True).then_inc(e_u[o], 1)
+            if i + 1 < len(RUNS):
+                out_of(o, V if UNP[o] == "V" else A)
+        freed[side] += len(pieces)
+        todo = []
 
     e_p, e_fv, e_fa, e_t, e_h, e_hq, e_y, e_ye = ([ev() for _ in range(4)] for _ in range(8))
     e_out = ev()
@@ -274,13 +428,30 @@ def rank_program(g, core, T, topo):
 
     def pick(o):
         to = T.gt if ROAD[o] == "P" else T.gl
-        for h, q, e in ((0, V, e_fv[o]), (1, A, e_fa[o])):
-            q.wait_ge(T.sem["bank%d" % o], freed)
-            copy(q, to[:, S * o + hs * h:S * o + hs * h + hs], T.dw[:, W * o:W * o + W].indirect(T.s16[:, 16 * h:16 * h + 16]), e)
+        cut = SPLIT[o]
+        if o in QUART:
+            e_a4 = [ev() for _ in range(4)]
+            for a in (0, 2, 1, 3):
+                q = V if a < 2 else A
+                for k in range(1 + TWO):
+                    q.wait_ge(T.sem["bank%d" % (4 * k + o)], freed[k])
+                copy(q, to[:, S * o + 128 * a:S * o + 128 * a + 128], T.dw[:, W * o:W * o + W].indirect(T.s16[:, 8 * a:8 * a + 8]), e_a4[a])
+            for a in (0, 2, 1, 3):
+                q = A if 10 * o + a in SELF else Y
+                q.wait_ge(e_a4[a], 1)
+                q.dma_start(T.gm[32 * a:32 * a + 32, S * o:S * o + S],
+                            to[:, S * o + 128 * a:S * o + 128 * a + 128]).then_inc(e_p[o], 16)
+            return
+        for q, lo, hi, e in ((V, 0, cut, e_fv[o]), (A, cut, S // 16, e_fa[o])):
+            for k in range(1 + TWO):
+                q.wait_ge(T.sem["bank%d" % (4 * k + o)], freed[k])
+            copy(q, to[:, S * o + 16 * lo:S * o + 16 * hi], T.dw[:, W * o:W * o + W].indirect(T.s16[:, lo:hi]), e)
         for a in range(4 * (ROAD[o] == "L")):
-            q = A if a == 3 and o in SELF else Y
-            if a % 2 == 0 or q is A:
-                q.wait_ge((e_fv, e_fa)[a // 2][o], 1)
+            q = A if 10 * o + a in SELF else Y
+            if 8 * a < cut:
+                q.wait_ge(e_fv[o], 1)
+            if 8 * a + 8 > cut:
+                q.wait_ge(e_fa[o], 1)
             q.dma_start(T.gm[32 * a:32 * a + 32, S * o:S * o + S],
                         to[:, S * o + 128 * a:S * o + 128 * a + 128]).then_inc(e_p[o], 16)
 
@@ -290,6 +461,22 @@ def rank_program(g, core, T, topo):
         b = 512 * ROAD[:o].count("P")
         for t in range(4):
             P.transpose(T.pst[:, b + t:b + 512:4], T.gt[:, S * o + t:S * o + S:4], T.ident[:]).then_inc(e_t[o], 1)
+
+    four = [T.psu[:, 1024:1152], T.psu[:, 1536:1664], T.pst[:, 512:640], T.psu[:, 512:640]]
+    e_four = [ev() for _ in range(4 * ("T" in TAIL))]
+    parts = [1 if road == "P" else 4 for road in ROAD]
+
+    def turn_apart(o):
+        parts[o] = 4
+        P.wait_ge(e_fv[o], 1)
+        P.wait_ge(e_fa[o], 1)
+        for t in range(4):
+            P.transpose(four[t], T.gt[:, S * o + t:S * o + S:4], T.ident[:]).then_inc(e_four[t], 1)
+
+    def part(o, ts, q):
+        for t in ts:
+            q.wait_ge(e_four[t], 1)
+            copy(q, T.ht[:, 512 * o + t:512 * o + 512:4], four[t], e_h[o])
 
     def turn_here(o):
         V.wait_ge(e_p[o], 64)
@@ -302,18 +489,20 @@ def rank_program(g, core, T, topo):
         copy(q, T.ht[:, 512 * o:512 * o + 512], T.pst[:, b:b + 512], e_h[o])
 
     def quant(o):
-        V.wait_ge(e_h[o], 1 if ROAD[o] == "P" else 4)
+        V.wait_ge(e_h[o], parts[o])
         V.quantize_mx(T.hq[:, 128 * o:128 * o + 128], T.hp[:, 128 * o:128 * o + 128],
                       T.ht[:, 512 * o:512 * o + 512]).then_inc(e_hq[o], 1)
 
-    def h_out(o):
-        Y.wait_ge(e_h[o], 1 if ROAD[o] == "P" else 4)
-        store(Y, T.h[:, 512 * o:512 * o + 512], T.ht[:, 512 * o:512 * o + 512])
+    def h_out(o, q=Y):
+        q.wait_ge(e_h[o], parts[o])
+        store(q, T.h[:, 512 * o:512 * o + 512], T.ht[:, 512 * o:512 * o + 512])
 
     banks = [T.psy[:, 0:NA], T.psy[:, 512:512 + NA], T.psu[:, 0:NA]]
     bank = {}
 
     def product(o):
+        if not bank:
+            P.wait_ge(e_aq, 1)
         bank[o] = banks[len(bank)] if len(bank) < 3 else T.psu[:, 512:512 + NA]
         P.wait_ge(e_hq[o], 1)
         P.matmul_mx(bank[o], T.hq[:, 128 * o:128 * o + 128], T.hp[:, 128 * o:128 * o + 128],
@@ -339,12 +528,14 @@ def rank_program(g, core, T, topo):
 
     if "P" in ROAD:
         P.wait_ge(e_id, 1)
-    P.wait_ge(e_aq, 1)
     A.wait_ge(e_s16, 1)
     V.wait_ge(e_s16, 1)
-    step = {"p": pick, "t": turn, "l": turn_here, "q": quant, "m": product, "e": empty, "y": y_out, "h": h_out, "z": last}
+    step = {"p": pick, "t": turn, "l": turn_here, "q": quant, "m": product, "e": empty, "y": y_out, "h": h_out, "z": last, "c": out_of,
+            "H": lambda o: h_out(o, A), "T": turn_apart, "a": lambda o: part(o, (0, 1, 2), A), "b": lambda o: part(o, (3,), V)}
     for w in TAIL.split():
-        if w[0] in "ey":
+        if w == "A":
+            quant_a()
+        elif w[0] in "eyc":
             step[w[0]](int(w[1]), V if w[2:] == "V" else A)
         else:
             step[w[0]](int(w[1]))

@@ -5,58 +5,58 @@ N, CAPP, NV, NA, S = 8, 96, 512, 256, 512
 W = N * CAPP
 LW = CAPP // 16
 COPY = ActivationFunctionType.Copy
-BATCH = ["p0", "f0 f1", "g0 g1 n1", "p1"]
-CALLS = [["c p0", "s p0"], ["c f0 f1", "s f0 f1"], ["c g0 g1 n1", "s g0 g1 n1"], ["c p1", "s p1"]]
-VIA = ""
-HAND = 8
-MOST = 8
-RUNS = ["n0 p0", "f0 f1", "n1", "g0 g1", "p1"]
-LISTS = ["p0", "f0 f1", "g0 g1 n1", "p1"]
-GATHER = ["VAVA", "VAVA", "VAVA", "VAAA"]
-NEAR = 4
+BATCH = ["f1 f0", "g0 p0", "g1", "n1|p1"]
+AFTER = ["c f1 f0, s f1 f0", "c g0 p0", "s g0 g1 p0, c g1", "c n1 p1, s n1 p1"]
+VIA = "lp1 cf0 sf0 cp0 sp0"
+RUNS = ["n0", "f1", "g0", "f0", "g1 n1", "p0 p1"]
+LISTS = ["f1 f0", "g0 p0 p1", "g1 n1"]
+LNEAR = 4
+GATHER = ["VAVA", "VAVA", "VAAA", "VAAA|VAVA"]
+OWN = "AAAV"
 ROAD = "PLLL"
-UORD = [1, 2, 0, 3]
-EARLY = 0
-GSEL = 3
-WHOLE = 1
-OWNQ = 0
-LATE = "P"
-HALF = 1
-TWO = 1
-OWN = "AAAA"
+ORDER = [1, 2, 0, 3]
+EARLY = 1
 SPLIT = [16, 16, 16, 16]
-QUART = [1, 3]
+QUART = {1: "VAVA", 3: "VAVA"}
 SELF = [33]
-UNP = "VAVA"
-TAIL = "c1V c2 p1 c0V c3 p2 p0 t0 p3 e0 H0 l1 h1 q1 m1 l2 h2 q2 q0 m2 y1 m0 y2 l3 q3 h3 y0 z3"
-NB = len(BATCH)
+STEPS = "k1 k2 k3 x04 o g0 g1 g2 g3 u01:0123:AVVA s a u22:0123:AVVA u33:0123:AVVA u44:0123:AVVA u55:0123 c0V c1 p1 c2V c3 p2 p0 t0 p3 e0 H0 l1 h1 q1 m1 l2 h2 q2 q0 m2 y1 m0 y2 l3 q3 h3 y0 z3"
+
+
+def each(words):
+    return words.replace("|", " ").split()
+
+
 GROUPS = [words for b in BATCH for words in b.split("|")]
-WIDE = [max(128, CAPP * len(b.replace("|", " ").split())) for b in BATCH] + [128]
+WIDE = [max(128, CAPP * len(each(b))) for b in BATCH]
 LS = 4 * LW
+GAP = 128 - CAPP
+TILES = [(o, m) for o in ORDER for m in range(4 if ROAD[o] == "R" else 1)]
+CALLS = [("l", c) for c in LISTS] + [(c[0], c[2:]) for calls in AFTER for c in calls.split(", ")]
+HANDS = [(kind, c) for kind, c in CALLS if any(kind + w in VIA for w in each(c))]
+SQ = S // 16
 
 SCRATCH = {
     "w32": ("sbuf", [128, N * LW], "int32"),
     "w16": ("sbuf", [128, N * LW], "uint16"),
-    "lst": ("sbuf", [128, LS * NB], "uint16"),
-    "s32": ("sbuf", [128, S // 16], "int32"),
-    "s16": ("sbuf", [128, S // 16], "uint16"),
+    "lst": ("sbuf", [128, LS * len(GROUPS)], "uint16"),
+    "s32": ("sbuf", [128, SQ + SQ // 4], "int32"),
+    "s16": ("sbuf", [128, SQ + SQ // 4], "uint16"),
     "vt": ("sbuf", [128, 4 * NV], "bfloat16"),
     "at": ("sbuf", [128, 4 * NA], "bfloat16"),
     "aq": ("sbuf", [128, NA], "float8_e4m3fn_x4"),
     "ap": ("sbuf", [128, NA], "uint8"),
     "mP": ("sbuf", [128, 128], "bfloat16"),
     "mL": ("sbuf", [128, 128], "bfloat16"),
-    "jL": ("sbuf", [128, 512], "bfloat16"),
-    "ones": ("sbuf", [128, 512], "bfloat16"),
+    "mR": ("sbuf", [128, 128], "bfloat16"),
     "onef": ("sbuf", [128, 128], "float32"),
-    "pi": ("sbuf", [128, 16], "float32"),
-    "et": ("sbuf", [128, 2048], "bfloat16"),
-    "eq": ("sbuf", [128, 512], "float8_e4m3fn_x4"),
-    "ep": ("sbuf", [128, 512], "uint8"),
+    "et": ("sbuf", [128, 512 * len(TILES)], "bfloat16"),
+    "eq": ("sbuf", [128, 128 * len(TILES)], "float8_e4m3fn_x4"),
+    "ep": ("sbuf", [128, 128 * len(TILES)], "uint8"),
     "ident": ("sbuf", [128, 128], "float32"),
-    "cq": ("sbuf", [128, W], "float8_e4m3fn_x4"),
-    "cp": ("sbuf", [128, W], "uint8"),
-    "dw": ("sbuf", [128, 4 * W], "bfloat16"),
+    "xo": ("sbuf", [128, 512], "bfloat16"),
+    "cq": ("sbuf", [128, W + GAP], "float8_e4m3fn_x4"),
+    "cp": ("sbuf", [128, W + GAP], "uint8"),
+    "dw": ("sbuf", [128, W * len(TILES)], "bfloat16"),
     "gt": ("sbuf", [128, 4 * S], "float32"),
     "gl": ("sbuf", [128, 4 * S], "bfloat16"),
     "gm": ("sbuf", [128, 4 * S], "bfloat16"),
@@ -64,17 +64,16 @@ SCRATCH = {
     "hq": ("sbuf", [128, S], "float8_e4m3fn_x4"),
     "hp": ("sbuf", [128, S], "uint8"),
     "yt": ("sbuf", [128, 4 * NA], "float32"),
-    "psu": ("psum", [128, 2048], "float32"),
-    "pst": ("psum", [128, 1024], "float32"),
-    "psy": ("psum", [128, 1024], "float32"),
+    "ps": ("psum", [128, 4096], "float32"),
 }
 for _i, _n in enumerate(WIDE):
     SCRATCH["x%d" % _i] = ("sbuf", [128, 4 * _n], "bfloat16")
     SCRATCH["q%d" % _i] = ("sbuf", [128, _n], "float8_e4m3fn_x4")
     SCRATCH["p%d" % _i] = ("sbuf", [128, _n], "uint8")
-NEV = 124
-SEMAPHORES = (["loc", "left", "via0", "via1"] + ["lst%d" % i for i in range(len(GROUPS))] + ["arr%d" % i for i in range(len(RUNS))]
-              + ["bank%d" % k for k in range(8)] + ["e%d" % k for k in range(NEV)])
+NEV = 100
+SEMAPHORES = (["loc"] + ["via%d" % k for k in range(len(HANDS))] + ["lst%d" % i for i in range(len(GROUPS))]
+              + ["arr%d" % i for i in range(len(RUNS))] + ["made%d" % k for k in range(8)] + ["free%d" % k for k in range(8)]
+              + ["e%d" % k for k in range(NEV)])
 
 
 KIN = {}
@@ -96,62 +95,98 @@ def learn(topo, cores):
 
 
 def named(r, words):
-    return [2 * KIN[r, w[0]] + (r + int(w[1])) % 2 for w in words.split()]
-
-
-def batches(r):
-    return [named(r, b.replace("|", " ")) for b in BATCH]
+    return [2 * KIN[r, w[0]] + (r + int(w[1])) % 2 for w in each(words)]
 
 
 def asked(r, words):
-    return [q for w in words.split() for q in range(N) if named(q, w) == [r]]
+    return [q for w in each(words) for q in range(N) if named(q, w) == [r]]
 
 
-def lanes(topo, cores, r, group, most=16, via=()):
-    off = [q for q in group if topo.chip(cores[r]) != topo.chip(cores[q]) and q not in via]
-    eng = topo.engines(cores[r], cores[(r + 2) % N])
-    wide = [1] * len(off)
-    k = 0
-    while off and sum(wide) + wide[k] <= len(eng) and wide[k] < most:
-        wide[k] *= 2
-        k = (k + 1) % len(off)
-    out = {q: eng[sum(wide[:k]):sum(wide[:k + 1])] for k, q in enumerate(off)}
-    rest = [e for e in topo.engines(cores[r], cores[named(r, "n1")[0]]) if e not in eng]
-    for k, q in enumerate([q for q in group if q not in out]):
-        out[q] = rest[NEAR * k:NEAR * k + NEAR]
-    return out
+def other(r, kind, w):
+    return (asked if kind == "l" else named)(r, w)[0]
 
 
 def helper(topo, cores, r):
-    can = [c for c in topo.cores_of(cores[r]) if topo.die(c) != topo.die(cores[r])
-           and all(topo.may_write(c, cores[q]) for s in (r - r % 2, r - r % 2 + 1) for q in named(s, VIA))]
-    return can[len(can) // 2 * (r % 2)]
+    can = [c for c in topo.cores_of(cores[r]) if topo.die(c) != topo.die(cores[r]) and all(topo.may_write(c, d) for d in cores)]
+    return can[r % 2]
 
 
-def hand_on(g, core, T, topo, cores, r):
-    sent = 0
-    for k, q in enumerate(named(r, VIA)):
-        at, eng = place(r, q), topo.engines(core, cores[q])[:HAND]
-        rid, pid, _ = topo.addr(cores[q])
-        g.wait_ge(T.sem["via%d" % k], NEAR)
-        g.remote_dma_fused([RemoteDMATransfer(
-            dst_ids=[DstId(rid=rid, pnc=pid)], dma_engine_mask=sum(1 << e for e in eng),
-            src=T.cq[:, CAPP * k:CAPP * k + CAPP].bitcast(dt.uint8), dst=T.cq[:, at:at + CAPP].bitcast(dt.uint8),
-            remote_sem=T.sem["arr%d" % [r in run for run in runs(q)].index(True)])], local_sem=T.sem.loc)
-        sent += len(eng)
-    g.wait_ge(T.sem.loc, sent)
+def shares(eng, n):
+    wide, k = [1] * n, 0
+    while n and sum(wide) + wide[k] <= len(eng):
+        wide[k] *= 2
+        k = (k + 1) % n
+    return [eng[sum(wide[:k]):sum(wide[:k + 1])] for k in range(n)]
+
+
+def lanes(topo, cores, r, kind, words):
+    out = topo.engines(cores[r], cores[named(r, "p0")[0]])
+    rest = [e for e in topo.engines(cores[r], cores[named(r, "n1")[0]]) if e not in out]
+    near = [w for w in each(words) if w[0] == "n" or kind + w in VIA]
+    off = [w for w in each(words) if w not in near]
+    if kind == "l":
+        done = [w for call in LISTS for w in each(call) if w[0] == "n" or kind + w in VIA]
+        on = [rest[LNEAR * done.index(w) % len(rest):][:LNEAR] for w in near]
+    else:
+        on = shares(rest, len(near))
+    return dict(zip(off + near, shares(out, len(off)) + on))
+
+
+def handed(topo, cores, r, kind, words):
+    mine = [w for w in each(words) if kind + w in VIA]
+    return dict(zip(mine, shares(topo.engines(helper(topo, cores, r), cores[other(r, kind, mine[0])]), len(mine))))
+
+
+def landing(topo, cores, r, kinds, words):
+    n = 0
+    for kind, call in CALLS:
+        for w in each(call):
+            if kind in kinds and w in words:
+                q = (named if kind == "l" else asked)(r, w)[0]
+                n += len((handed if kind + w in VIA else lanes)(topo, cores, q, kind, call)[w])
+    return n
 
 
 def runs(r):
-    out = []
-    for words in RUNS:
-        run = asked(r, words)
-        out.append(sorted(run, key=lambda q: ([s // 2 for s in run].index(q // 2), q)))
-    return out
+    return [sorted(asked(r, words)) for words in RUNS]
 
 
-def place(s, r):
-    return CAPP * [q for run in runs(r) for q in run].index(s)
+def place(q, r):
+    return CAPP * [x for run in runs(r) for x in run].index(q) + GAP * (q != r)
+
+
+def where(T, r, kind, w):
+    q = other(r, kind, w)
+    if kind == "l":
+        i = [w in words for words in GROUPS].index(True)
+        k = LS * i + LW * each(GROUPS[i]).index(w)
+        return T.w16[:, LW * q:LW * q + LW], T.w16[:, LW * q:LW * q + LW], T.lst[:, k:k + LW], T.sem["lst%d" % i]
+    i = [w in b for b in BATCH].index(True)
+    k, at, rest = CAPP * each(BATCH[i]).index(w), place(r, q), CAPP * q
+    sem = T.sem["arr%d" % [w in words for words in RUNS].index(True)]
+    if kind == "c":
+        return (T["q%d" % i][:, k:k + CAPP].bitcast(dt.uint8), T.cq[:, rest:rest + CAPP].bitcast(dt.uint8),
+                T.cq[:, at:at + CAPP].bitcast(dt.uint8), sem)
+    return T["p%d" % i][:, k:k + CAPP], T.cp[:, rest:rest + CAPP], T.cp[:, at:at + CAPP], sem
+
+
+def transfer(topo, core, eng, src, dst, sem):
+    rid, pid, _ = topo.addr(core)
+    return RemoteDMATransfer(dst_ids=[DstId(rid=rid, pnc=pid)], dma_engine_mask=sum(1 << e for e in eng), src=src, dst=dst,
+                             remote_sem=sem)
+
+
+def hand_on(g, T, topo, cores, r):
+    sent = 0
+    for j, (kind, call) in enumerate(HANDS):
+        g.wait_ge(T.sem["via%d" % j], sum(len(e) for w, e in lanes(topo, cores, r, kind, call).items() if kind + w in VIA))
+        tr = []
+        for w, eng in handed(topo, cores, r, kind, call).items():
+            _, rest, dst, sem = where(T, r, kind, w)
+            tr.append(transfer(topo, cores[other(r, kind, w)], eng, rest, dst, sem))
+            sent += len(eng)
+        g.remote_dma_fused(tr, local_sem=T.sem.loc)
+    g.wait_ge(T.sem.loc, sent)
 
 
 def rank_program(g, core, T, topo):
@@ -159,12 +194,12 @@ def rank_program(g, core, T, topo):
     learn(topo, cores)
     r = T.rank_of(core)
     if r is None:
-        for s in range(N):
-            if VIA and core == helper(topo, cores, s):
-                hand_on(g, core, T, topo, cores, s)
+        for q in range(N):
+            if core == helper(topo, cores, q):
+                hand_on(g, T, topo, cores, q)
         return
     V, A, P, Y = g.vector, g.scalar, g.tensor, g.sync
-    used, nloc = [0], {"loc": 0, "left": 0}
+    used, nloc = [0], [0]
 
     def ev():
         used[0] += 1
@@ -176,366 +211,274 @@ def rank_program(g, core, T, topo):
         else:
             A.activation(out, src, COPY).then_inc(sem, 1)
 
-    def send(group, piece, sem, gone, most=16, via=()):
-        eng = lanes(topo, cores, r, group, most, via)
-        tr = []
-        for q in group:
-            rid, pid, _ = topo.addr(helper(topo, cores, r) if q in via else cores[q])
-            src, dst = piece(q)
-            if q in via:
-                k = via.index(q)
-                dst = T.cq[:, CAPP * k:CAPP * k + CAPP].bitcast(dt.uint8)
-            tr.append(RemoteDMATransfer(dst_ids=[DstId(rid=rid, pnc=pid)], dma_engine_mask=sum(1 << e for e in eng[q]), src=src,
-                                        dst=dst, remote_sem=T.sem["via%d" % k] if q in via else sem(q)))
-            nloc[gone] += len(eng[q])
-        g.remote_dma_fused(tr, local_sem=T.sem[gone])
+    def send(kind, words):
+        eng, tr = lanes(topo, cores, r, kind, words), []
+        for w in each(words):
+            src, rest, dst, sem = where(T, r, kind, w)
+            if kind + w in VIA:
+                tr.append(transfer(topo, helper(topo, cores, r), eng[w], src, rest, T.sem["via%d" % HANDS.index((kind, words))]))
+            else:
+                tr.append(transfer(topo, cores[other(r, kind, w)], eng[w], src, dst, sem))
+            nloc[0] += len(eng[w])
+        g.remote_dma_fused(tr, local_sem=T.sem.loc)
 
     e_w, e_v, e_s, e_a = ev(), ev(), ev(), ev()
-    for k in range(4 if HALF else 8):
+    for k in range(4):
         (Y if k % 2 == 0 else A).dma_start(T.w32[16 * k:16 * k + 16, :], T.want[:]).then_inc(e_w, 16)
     Y.dma_start(T.vt[:], T.v[:]).then_inc(e_v, 16)
-    for k in range(8):
-        Y.dma_start(T.s32[16 * k:16 * k + 16, :], T.slot[:]).then_inc(e_s, 16)
     Y.dma_start(T.at[:], T.a[:]).then_inc(e_a, 16)
+    for k in range(8):
+        Y.dma_start(T.s32[16 * k:16 * k + 16, 0:SQ], T.slot[:]).then_inc(e_s, 16)
+    for k in range(8 * ("R" in ROAD)):
+        Y.dma_start(T.s32[16 * k:16 * k + 16, SQ:SQ + 8], T.slot[:, 8 * (k // 2):8 * (k // 2) + 8]).then_inc(e_s, 16)
 
-    e_z, e_c = ev(), ev()
-    e_i, e_eq, e_id = {road: ev() for road in "PL"}, ev(), ev()
+    e_z, e_c, e_id, e_one = (ev() for _ in range(4))
+    e_m = {road: ev() for road in "LPR"}
+    e_e, e_eq = [ev() for _ in TILES], {}
 
-    def rows(road):
-        g.iota(T["m" + road][:], {"P": [[1, 128]], "L": [[1, 32], [32, 4]]}[road], 0, 0,
-               allow_small_or_imprecise_dtypes=True).then_inc(e_i[road], 1)
-
-    e_e = [ev() for _ in range(4)]
-
-    def onehot(o):
-        V.wait_ge(e_i[ROAD[o]], 1)
-        if WHOLE and ROAD[o] == "L":
-            V.tensor_scalar(T.et[:, 512 * o:512 * o + 512], T.jL[:], 192.0 - 128 * o, None,
-                            AluOpType.is_equal).then_inc(e_e[o], 4)
-            return
-        V.wait_ge(e_pi, 1)
+    def onehot(j):
+        o, m = TILES[j]
+        V.wait_ge(e_m[ROAD[o]], 1)
         for t in range(4):
-            V.tensor_scalar(T.et[:, 512 * o + t:512 * o + 512:4], T["m" + ROAD[o]][:], T.pi[:, 4 * o + t:4 * o + t + 1],
-                            None, AluOpType.is_equal).then_inc(e_e[o], 1)
-
-    def swapped(o):
-        A.wait_ge(e_e[o - 2], 4)
-        for h in range(2):
-            A.activation(T.et[64 * h:64 * h + 64, 512 * o:512 * o + 512],
-                         T.et[64 - 64 * h:128 - 64 * h, 512 * o - 1024:512 * o - 512], COPY).then_inc(e_e[o], 2)
+            V.tensor_scalar(T.et[:, 512 * j + t:512 * j + 512:4], T["m" + ROAD[o]][:], 240.0 - 128 * o - 32 * m + t, None,
+                            AluOpType.is_equal).then_inc(e_e[j], 1)
 
     def pack(a, b):
-        for o in range(a, b):
-            V.wait_ge(e_e[o], 4)
-        V.quantize_mx(T.eq[:, 128 * a:128 * b], T.ep[:, 128 * a:128 * b], T.et[:, 512 * a:512 * b]).then_inc(e_eq, 1)
+        e = ev()
+        for j in range(a, b):
+            V.wait_ge(e_e[j], 4)
+            e_eq[j] = e
+        V.quantize_mx(T.eq[:, 128 * a:128 * b], T.ep[:, 128 * a:128 * b], T.et[:, 512 * a:512 * b]).then_inc(e, 1)
 
-    e_pi = ev()
-    if WHOLE:
-        g.iota(T.jL[:], [[1, 32], [32, 4], [-1, 4]], 192, -4, allow_small_or_imprecise_dtypes=True).then_inc(e_i["L"], 1)
-    else:
-        g.iota(T.pi[:], [[-128, 4], [1, 4]], 0, 4, allow_small_or_imprecise_dtypes=True).then_inc(e_pi, 1)
-        for road in "LP":
-            rows(road)
-    nz = 0
-    for i, n in enumerate([CAPP * len(grp) for grp in batches(r)] + [CAPP]):
-        if n < 128:
-            V.memset(T["x%d" % i][:, 4 * n:512], 0.0).then_inc(e_z, 1)
-            nz += 1
-    e_one = ev()
-    if GSEL:
-        A.wait_ge(e_i["L"], 1)
-        for s in range(4):
-            A.activation(T.mP[:, 32 * s:32 * s + 32], T.jL[:, 4 * s:512:16], COPY).then_inc(e_i["P"], 1)
+    for road, pattern in (("L", [[1, 32], [32, 4]]), ("P", [[1, 128]]), ("R", [[0, 4], [1, 32]])):
+        if road in ROAD:
+            g.iota(T["m" + road][:], pattern, 240, -4, allow_small_or_imprecise_dtypes=True).then_inc(e_m[road], 1)
+    narrow = [T.xo] + [T["x%d" % i] for i, b in enumerate(BATCH) if len(each(b)) == 1]
+    for x in narrow:
+        V.memset(x[:, 4 * CAPP:512], 0.0).then_inc(e_z, 1)
+    if "P" in ROAD:
         V.memset(T.onef[:], 1.0).then_inc(e_one, 1)
-    if EARLY:
-        onehot(1)
-        swapped(3)
+    for j in range(EARLY):
+        onehot(j)
 
-    V.wait_ge(e_w, 64 if HALF else 128)
-    for h in range(1 + HALF):
-        n = 64 if HALF else 128
-        V.tensor_scalar(T.w16[n * h:n * h + n, :], T.w32[0:n, :], 0.0, 4.0, AluOpType.max, AluOpType.mult).then_inc(e_c, 1)
-    g.wait_ge(e_c, 1 + HALF)
-
-    def list_piece(q):
-        i = [r in b for b in batches(q)].index(True)
-        k = LS * i + LW * batches(q)[i].index(r)
-        return T.w16[:, LW * q:LW * q + LW], T.lst[:, k:k + LW]
-
-    def lists(words, gone):
-        send(asked(r, words), list_piece, lambda q: T.sem["lst%d" % [r in named(q, w) for w in GROUPS].index(True)], gone, MOST)
-
+    V.wait_ge(e_w, 64)
+    for h in range(2):
+        V.tensor_scalar(T.w16[64 * h:64 * h + 64, :], T.w32[0:64, :], 0.0, 4.0, AluOpType.max, AluOpType.mult).then_inc(e_c, 1)
+    g.wait_ge(e_c, 2)
     for call in LISTS:
-        lists(call, "left")
-    if WHOLE and not GSEL:
-        g.iota(T.pi[:], [[-128, 4], [1, 4]], 0, 4, allow_small_or_imprecise_dtypes=True).then_inc(e_pi, 1)
-        rows("P")
-
-    def tile_p():
-        if GSEL:
-            V.wait_ge(e_i["P"], 4)
-            for t in range(4):
-                V.tensor_scalar(T.et[:, t:512:4], T.mP[:], 192.0 + t, None, AluOpType.is_equal).then_inc(e_e[0], 1)
-            return
-        onehot(0)
-        V.tensor_scalar(T.ident[:], T.mP[:], 4.0, T.pi[:, 0:1], AluOpType.mult, AluOpType.is_equal).then_inc(e_id, 1)
-
-    if not EARLY:
-        onehot(1)
-        onehot(3)
-    onehot(2)
-    if not LATE:
-        tile_p()
-    pack(1 if LATE else 0, 4)
-
-    e_own = ev()
-
-    e_og = ev()
+        send("l", call)
+    V.wait_ge(e_z, len(narrow))
+    e_own, e_s16, e_aq = ev(), ev(), ev()
 
     def own():
-        x = T["x%d" % NB]
+        e = ev()
+        for q in (V, A):
+            q.wait_ge(e_c, 2)
+            q.wait_ge(e_v, 16)
         for t in range(4):
-            copy(V if OWN[t] == "V" else A, x[:, t:4 * CAPP:4], T.vt[:, t:4 * NV].indirect(T.w16[:, LW * r:LW * r + LW]), e_og)
-        if not OWNQ:
-            own_codes()
+            copy(V if OWN[t] == "V" else A, T.xo[:, t:4 * CAPP:4], T.vt[:, t:4 * NV].indirect(T.w16[:, LW * r:LW * r + LW]), e)
+        V.wait_ge(e, 4)
+        V.quantize_mx(T.cq[:, 0:128], T.cp[:, 0:128], T.xo[:]).then_inc(e_own, 1)
 
-    def own_codes():
-        e_q = ev()
-        x, qb, pb = (T["%s%d" % (c, NB)] for c in "xqp")
-        V.wait_ge(e_og, 4)
-        V.quantize_mx(qb[:], pb[:], x[:]).then_inc(e_q, 1)
-        Y.wait_ge(e_q, 1)
-        at = place(r, r)
-        Y.dma_start(T.cq[:, at:at + CAPP].bitcast(dt.uint8), qb[:, 0:CAPP].bitcast(dt.uint8)).then_inc(e_own, 16)
-        Y.dma_start(T.cp[:, at:at + CAPP], pb[:, 0:CAPP]).then_inc(e_own, 16)
-
-    for q in (V, A):
-        q.wait_ge(e_c, 1 + HALF)
-        q.wait_ge(e_v, 16)
-    V.wait_ge(e_z, nz)
-    Y.wait_ge(T.sem.left, nloc["left"])
-    if OWN[4:] == "":
-        own()
-
-    def made(q):
-        i = [q in b for b in batches(r)].index(True)
-        return i, CAPP * batches(r)[i].index(q), place(r, q)
-
-    def codes(q):
-        i, k, at = made(q)
-        return T["q%d" % i][:, k:k + CAPP].bitcast(dt.uint8), T.cq[:, at:at + CAPP].bitcast(dt.uint8)
-
-    def planes(q):
-        i, k, at = made(q)
-        return T["p%d" % i][:, k:k + CAPP], T.cp[:, at:at + CAPP]
-
-    for i, grp in enumerate(batches(r)):
+    def serve(i):
         x, qb, pb = (T["%s%d" % (c, i)] for c in "xqp")
         e_g, e_q = ev(), ev()
-        for words in BATCH[i].split("|"):
-            k, part = GROUPS.index(words), named(r, words)
-            lo, hi = grp.index(part[0]), grp.index(part[-1]) + 1
-            need = sum(len(lanes(topo, cores, q, asked(q, call), MOST)[r])
-                       for call in LISTS for q in named(r, call) if q in part)
-            V.wait_ge(T.sem["lst%d" % k], need)
-            A.wait_ge(T.sem["lst%d" % k], need)
+        lo = 0
+        for words, who in zip(BATCH[i].split("|"), GATHER[i].split("|")):
+            k, n = GROUPS.index(words), len(each(words))
+            for q in (V, A):
+                q.wait_ge(T.sem["lst%d" % k], landing(topo, cores, r, "l", words))
             for t in range(4):
-                copy(V if GATHER[k][t] == "V" else A, x[:, 4 * CAPP * lo + t:4 * CAPP * hi:4],
-                     T.vt[:, t:4 * NV].indirect(T.lst[:, LS * i + LW * lo:LS * i + LW * hi]), e_g)
+                copy(V if who[t] == "V" else A, x[:, 4 * CAPP * lo + t:4 * CAPP * (lo + n):4],
+                     T.vt[:, t:4 * NV].indirect(T.lst[:, LS * k:LS * k + LW * n]), e_g)
+            lo += n
         V.wait_ge(e_g, 4 * len(BATCH[i].split("|")))
         V.quantize_mx(qb[:], pb[:], x[:]).then_inc(e_q, 1)
-        if i + 1 == OWNQ:
-            own_codes()
         g.wait_ge(e_q, 1)
-        for call in CALLS[i]:
-            send(named(r, call[2:]), codes if call[0] == "c" else planes,
-                 lambda q: T.sem["arr%d" % [r in run for run in runs(q)].index(True)], "loc", 8,
-                 named(r, VIA) if call[0] == "c" else ())
-        if GSEL and i == GSEL:
-            g.wait_ge(e_one, 1)
-            g.affine_select(T.ident[:], T.onef[:], [[-1, 128]], AluOpType.is_equal, 0.0, 0, 1).then_inc(e_id, 1)
-    g.wait_ge(T.sem.loc, nloc["loc"])
+        for call in AFTER[i].split(", "):
+            send(call[0], call[2:])
+        if i + 1 == len(BATCH):
+            if "P" in ROAD:
+                g.wait_ge(e_one, 1)
+                g.affine_select(T.ident[:], T.onef[:], [[-1, 128]], AluOpType.is_equal, 0.0, 0, 1).then_inc(e_id, 1)
+            g.wait_ge(T.sem.loc, nloc[0])
 
-    e_s16, e_aq = ev(), ev()
-    if LATE:
-        tile_p()
-        pack(0, 1)
-    if OWN[4:] != "":
-        own()
-    V.wait_ge(e_s, 128)
-    V.tensor_copy(T.s16[:], T.s32[:]).then_inc(e_s16, 1)
+    def slots():
+        n = SQ + 8 * ("R" in ROAD)
+        V.wait_ge(e_s, 128 + 128 * ("R" in ROAD))
+        V.tensor_copy(T.s16[:, 0:n], T.s32[:, 0:n]).then_inc(e_s16, 1)
 
     def quant_a():
         V.wait_ge(e_a, 16)
         V.quantize_mx(T.aq[:], T.ap[:], T.at[:]).then_inc(e_aq, 1)
 
-    if "A" not in TAIL:
-        quant_a()
+    idle, made, free, seen = list(range(8)), [0] * 8, [0] * 8, {}
 
-    freed = [0, 0]
-    P.wait_ge(e_eq, 2 if LATE else 1)
-    todo, e_u = [], {}
+    def wait(q, sem, n):
+        name = "V" if q is V else "A" if q is A else "P"
+        if seen.get((name, sem), 0) < n:
+            q.wait_ge(T.sem[sem], n)
+            seen[name, sem] = n
 
-    def out_of(o, q):
-        q.wait_ge(e_u[o], 1)
+    def take():
+        b = idle.pop(0)
+        wait(P, "free%d" % b, free[b])
+        made[b] += 1
+        return b
+
+    def drain(q, b, n, out, lo, hi):
+        wait(q, "made%d" % b, n)
+        copy(q, out, T.ps[:, 512 * b + lo:512 * b + hi], T.sem["free%d" % b])
+        free[b] += 1
+        if b not in idle:
+            idle.append(b)
+        return "free%d" % b, free[b]
+
+    late, full = [], [[] for _ in TILES]
+
+    def out_of(job, q):
+        j, b, n, first, pieces = job
         for piece in pieces:
-            c, d, n = place(piece[0], r) - first, W * o + CAPP * piece[0], CAPP * len(piece)
-            copy(q, T.dw[:, d:d + n], in_bank(4 * side + o, c, c + n), T.sem["bank%d" % (4 * side + o)])
+            c, d = place(piece[0], r) - first, W * j + CAPP * piece[0]
+            full[j].append(drain(q, b, n, T.dw[:, d:d + CAPP * len(piece)], c, c + CAPP * len(piece)))
 
-    def in_bank(k, a, b):
-        return (T.psu, T.psu, T.pst, T.psy)[k // 2][:, 512 * (k if k < 4 else k % 2) + a:512 * (k if k < 4 else k % 2) + b]
-
-    for i, run in enumerate(runs(r)):
-        if r in run:
-            P.wait_ge(e_own, 32)
-        need = 0
-        for q in run:
-            for call in [call for calls in CALLS for call in calls if r in named(q, call[2:])]:
-                via = named(q, VIA) if call[0] == "c" else ()
-                need += HAND if r in via else len(lanes(topo, cores, q, named(q, call[2:]), 8, via)[r])
-        P.wait_ge(T.sem["arr%d" % i], need)
-        todo += run
-        end = place(todo[-1], r) + CAPP
-        if end < 128:
-            continue
-        first = min(place(todo[0], r), end - 128)
-        side = (len(RUNS) - 1 - i) % 2 * TWO
-        pieces = [[q] for q in todo[:1]]
-        for q in todo[1:]:
-            if q == pieces[-1][-1] + 1:
+    def unpack(lo, hi, tiles, who):
+        ranks = [q for run in runs(r)[lo:hi + 1] for q in run]
+        for i in range(lo, hi + 1):
+            if i == 0:
+                P.wait_ge(e_own, 1)
+            else:
+                wait(P, "arr%d" % i, landing(topo, cores, r, "cs", RUNS[i]))
+        end = max(128, place(ranks[-1], r) + CAPP)
+        first = min(place(ranks[0], r), end - 128)
+        pieces = [ranks[:1]]
+        for q in ranks[1:]:
+            if q == pieces[-1][-1] + 1 and pieces[-1][-1] != r:
                 pieces[-1].append(q)
             else:
                 pieces.append([q])
-        for o in UORD:
-            e_u[o] = ev()
-            if freed[side]:
-                P.wait_ge(T.sem["bank%d" % (4 * side + o)], freed[side])
-            P.matmul_mx(in_bank(4 * side + o, 0, end - first), T.eq[:, 128 * o:128 * o + 128],
-                        T.ep[:, 128 * o:128 * o + 128], T.cq[:, first:end], T.cp[:, first:end], True, True).then_inc(e_u[o], 1)
-            if i + 1 < len(RUNS):
-                out_of(o, V if UNP[o] == "V" else A)
-        freed[side] += len(pieces)
-        todo = []
+        for k, j in enumerate(tiles):
+            if e_eq[j] is not None:
+                P.wait_ge(e_eq[j], 1)
+                e_eq[j] = None
+            b = take()
+            P.matmul_mx(T.ps[:, 512 * b:512 * b + end - first], T.eq[:, 128 * j:128 * j + 128], T.ep[:, 128 * j:128 * j + 128],
+                        T.cq[:, first:end], T.cp[:, first:end], True, True).then_inc(T.sem["made%d" % b], 1)
+            job = j, b, made[b], first, pieces
+            if k < len(who):
+                out_of(job, V if who[k] == "V" else A)
+            else:
+                late.append(job)
 
-    e_p, e_fv, e_fa, e_t, e_h, e_hq, e_y, e_ye = ([ev() for _ in range(4)] for _ in range(8))
+    e_p, e_fv, e_fa, e_h, e_hq = ([ev() for _ in range(4)] for _ in range(5))
     e_out = ev()
     nout = [0]
-    hs = S // 2
 
     def store(q, out, src):
         q.dma_start(out, src).then_inc(e_out, 16)
         nout[0] += 16
 
+    def window(q, j, lo, hi):
+        q.wait_ge(e_s16, 1)
+        for sem, n in full[j][::-1]:
+            wait(q, sem, n)
+        return T.dw[:, W * j:W * j + W].indirect(T.s16[:, lo:hi])
+
+    def fold(o, a, q):
+        q.dma_start(T.gm[32 * a:32 * a + 32, S * o:S * o + S],
+                    T.gl[:, S * o + 128 * a:S * o + 128 * a + 128]).then_inc(e_p[o], 16)
+
     def pick(o):
-        to = T.gt if ROAD[o] == "P" else T.gl
-        cut = SPLIT[o]
-        if o in QUART:
-            e_a4 = [ev() for _ in range(4)]
-            for a in (0, 2, 1, 3):
-                q = V if a < 2 else A
-                for k in range(1 + TWO):
-                    q.wait_ge(T.sem["bank%d" % (4 * k + o)], freed[k])
-                copy(q, to[:, S * o + 128 * a:S * o + 128 * a + 128], T.dw[:, W * o:W * o + W].indirect(T.s16[:, 8 * a:8 * a + 8]), e_a4[a])
-            for a in (0, 2, 1, 3):
-                q = A if 10 * o + a in SELF else Y
-                q.wait_ge(e_a4[a], 1)
-                q.dma_start(T.gm[32 * a:32 * a + 32, S * o:S * o + S],
-                            to[:, S * o + 128 * a:S * o + 128 * a + 128]).then_inc(e_p[o], 16)
+        to, j, cut = T.gt if ROAD[o] == "P" else T.gl, TILES.index((o, 0)), SPLIT[o]
+        if ROAD[o] == "R":
+            for m in range(4):
+                q = V if QUART[o][m] == "V" else A
+                copy(q, T.gm[:, S * o + 128 * m:S * o + 128 * m + 128], window(q, j + m, SQ, SQ + 8), e_p[o])
             return
-        for q, lo, hi, e in ((V, 0, cut, e_fv[o]), (A, cut, S // 16, e_fa[o])):
-            for k in range(1 + TWO):
-                q.wait_ge(T.sem["bank%d" % (4 * k + o)], freed[k])
-            copy(q, to[:, S * o + 16 * lo:S * o + 16 * hi], T.dw[:, W * o:W * o + W].indirect(T.s16[:, lo:hi]), e)
+        if o in QUART:
+            e4 = [ev() for _ in range(4)]
+            for a in range(4):
+                q = V if QUART[o][a] == "V" else A
+                copy(q, to[:, S * o + 128 * a:S * o + 128 * a + 128], window(q, j, 8 * a, 8 * a + 8), e4[a])
+            for a in range(4):
+                q = A if 10 * o + a in SELF else Y
+                q.wait_ge(e4[a], 1)
+                fold(o, a, q)
+            return
+        for q, lo, hi, e in ((V, 0, cut, e_fv[o]), (A, cut, SQ, e_fa[o])):
+            copy(q, to[:, S * o + 16 * lo:S * o + 16 * hi], window(q, j, lo, hi), e)
         for a in range(4 * (ROAD[o] == "L")):
             q = A if 10 * o + a in SELF else Y
             if 8 * a < cut:
                 q.wait_ge(e_fv[o], 1)
             if 8 * a + 8 > cut:
                 q.wait_ge(e_fa[o], 1)
-            q.dma_start(T.gm[32 * a:32 * a + 32, S * o:S * o + S],
-                        to[:, S * o + 128 * a:S * o + 128 * a + 128]).then_inc(e_p[o], 16)
+            fold(o, a, q)
+
+    held, done = {}, {o: [] for o in range(4)}
 
     def turn(o):
+        P.wait_ge(e_id, 1)
         P.wait_ge(e_fv[o], 1)
         P.wait_ge(e_fa[o], 1)
-        b = 512 * ROAD[:o].count("P")
+        held[o] = []
         for t in range(4):
-            P.transpose(T.pst[:, b + t:b + 512:4], T.gt[:, S * o + t:S * o + S:4], T.ident[:]).then_inc(e_t[o], 1)
+            b = take()
+            P.transpose(T.ps[:, 512 * b:512 * b + 128], T.gt[:, S * o + t:S * o + S:4], T.ident[:]).then_inc(T.sem["made%d" % b], 1)
+            held[o].append((b, made[b]))
 
-    four = [T.psu[:, 1024:1152], T.psu[:, 1536:1664], T.pst[:, 512:640], T.psu[:, 512:640]]
-    e_four = [ev() for _ in range(4 * ("T" in TAIL))]
-    parts = [1 if road == "P" else 4 for road in ROAD]
-
-    def turn_apart(o):
-        parts[o] = 4
-        P.wait_ge(e_fv[o], 1)
-        P.wait_ge(e_fa[o], 1)
-        for t in range(4):
-            P.transpose(four[t], T.gt[:, S * o + t:S * o + S:4], T.ident[:]).then_inc(e_four[t], 1)
-
-    def part(o, ts, q):
-        for t in ts:
-            q.wait_ge(e_four[t], 1)
-            copy(q, T.ht[:, 512 * o + t:512 * o + 512:4], four[t], e_h[o])
+    def empty(o, q):
+        for t, (b, n) in enumerate(held[o]):
+            done[o].append(drain(q, b, n, T.ht[:, 512 * o + t:512 * o + 512:4], 0, 128))
 
     def turn_here(o):
-        V.wait_ge(e_p[o], 64)
+        V.wait_ge(e_p[o], 4 if ROAD[o] == "R" else 64)
         for t in range(4):
             V.transpose(T.ht[:, 512 * o + t:512 * o + 512:4], T.gm[:, S * o + t:S * o + S:4]).then_inc(e_h[o], 1)
 
-    def empty(o, q):
-        q.wait_ge(e_t[o], 4)
-        b = 512 * ROAD[:o].count("P")
-        copy(q, T.ht[:, 512 * o:512 * o + 512], T.pst[:, b:b + 512], e_h[o])
+    def turned(q, o):
+        if ROAD[o] != "P":
+            q.wait_ge(e_h[o], 4)
+        for sem, n in done[o]:
+            q.wait_ge(T.sem[sem], n)
 
     def quant(o):
-        V.wait_ge(e_h[o], parts[o])
+        turned(V, o)
         V.quantize_mx(T.hq[:, 128 * o:128 * o + 128], T.hp[:, 128 * o:128 * o + 128],
                       T.ht[:, 512 * o:512 * o + 512]).then_inc(e_hq[o], 1)
 
     def h_out(o, q=Y):
-        q.wait_ge(e_h[o], parts[o])
+        turned(q, o)
         store(q, T.h[:, 512 * o:512 * o + 512], T.ht[:, 512 * o:512 * o + 512])
 
-    banks = [T.psy[:, 0:NA], T.psy[:, 512:512 + NA], T.psu[:, 0:NA]]
-    bank = {}
-
-    def product(o):
-        if not bank:
-            P.wait_ge(e_aq, 1)
-        bank[o] = banks[len(bank)] if len(bank) < 3 else T.psu[:, 512:512 + NA]
+    def product(o, lo=0, hi=NA):
+        P.wait_ge(e_aq, 1)
         P.wait_ge(e_hq[o], 1)
-        P.matmul_mx(bank[o], T.hq[:, 128 * o:128 * o + 128], T.hp[:, 128 * o:128 * o + 128],
-                    T.aq[:], T.ap[:], True, True).then_inc(e_y[o], 1)
+        b = take()
+        P.matmul_mx(T.ps[:, 512 * b:512 * b + hi - lo], T.hq[:, 128 * o:128 * o + 128], T.hp[:, 128 * o:128 * o + 128],
+                    T.aq[:, lo:hi], T.ap[:, lo:hi], True, True).then_inc(T.sem["made%d" % b], 1)
+        held[o] = b, made[b]
 
-    def y_out(o, q):
-        q.wait_ge(e_y[o], 1)
-        copy(q, T.yt[:, NA * o:NA * o + NA], bank[o], e_ye[o])
-        Y.wait_ge(e_ye[o], 1)
-        store(Y, T.y[:, NA * o:NA * o + NA], T.yt[:, NA * o:NA * o + NA])
+    def y_out(o, q, d=Y, lo=0, hi=NA):
+        sem, n = drain(q, *held[o], T.yt[:, NA * o + lo:NA * o + hi], 0, hi - lo)
+        d.wait_ge(T.sem[sem], n)
+        store(d, T.y[:, NA * o + lo:NA * o + hi], T.yt[:, NA * o + lo:NA * o + hi])
 
     def last(o):
-        P.wait_ge(e_hq[o], 1)
         for h, q, d in ((0, V, Y), (1, A, A)):
-            e_m, e_o = ev(), ev()
-            b, c = T.psu[:, 512 * (h + 1):512 * (h + 1) + 128], NA * o + 128 * h
-            P.matmul_mx(b, T.hq[:, 128 * o:128 * o + 128], T.hp[:, 128 * o:128 * o + 128],
-                        T.aq[:, 128 * h:128 * h + 128], T.ap[:, 128 * h:128 * h + 128], True, True).then_inc(e_m, 1)
-            q.wait_ge(e_m, 1)
-            copy(q, T.yt[:, c:c + 128], b, e_o)
-            d.wait_ge(e_o, 1)
-            store(d, T.y[:, c:c + 128], T.yt[:, c:c + 128])
+            product(o, 128 * h, 128 * h + 128)
+            y_out(o, q, d, 128 * h, 128 * h + 128)
 
-    if "P" in ROAD:
-        P.wait_ge(e_id, 1)
-    A.wait_ge(e_s16, 1)
-    V.wait_ge(e_s16, 1)
-    step = {"p": pick, "t": turn, "l": turn_here, "q": quant, "m": product, "e": empty, "y": y_out, "h": h_out, "z": last, "c": out_of,
-            "H": lambda o: h_out(o, A), "T": turn_apart, "a": lambda o: part(o, (0, 1, 2), A), "b": lambda o: part(o, (3,), V)}
-    for w in TAIL.split():
-        if w == "A":
-            quant_a()
-        elif w[0] in "eyc":
+    step = {"p": pick, "l": turn_here, "q": quant, "m": product, "y": y_out, "h": h_out, "z": last, "e": empty, "k": onehot,
+            "c": lambda k, q: out_of(late[k], q), "H": lambda o: h_out(o, A), "t": turn, "g": serve}
+    for w in STEPS.split():
+        if w in "aso":
+            {"a": quant_a, "s": slots, "o": own}[w]()
+        elif w[0] == "x":
+            pack(int(w[1]), int(w[2]))
+        elif w[0] == "u":
+            unpack(int(w[1]), int(w[2]), [int(j) for j in w.split(":")[1]], w.split(":")[2] if w.count(":") > 1 else "")
+        elif w[0] in "yce":
             step[w[0]](int(w[1]), V if w[2:] == "V" else A)
         else:
             step[w[0]](int(w[1]))

from concourse.bass import DstId, RemoteDMATransfer
from concourse.mybir import dt, AluOpType, ActivationFunctionType

N, CAPP, NV, NA, S = 8, 96, 512, 256, 512
W = N * CAPP
LW = CAPP // 16
COPY = ActivationFunctionType.Copy
BATCH = ["f1 f0", "g0 p0", "g1", "n1|p1"]
AFTER = ["c f1 f0, s f1 f0", "c g0 p0", "s g0 g1 p0, c g1", "c n1 p1, s n1 p1"]
VIA = "lp1 cf0 sf0 cp0 sp0"
RUNS = ["n0", "f1", "g0", "f0", "g1 n1", "p0 p1"]
LISTS = ["f1 f0", "g0 p0 p1", "g1 n1"]
LNEAR = 4
GATHER = ["VAVA", "VAVA", "VAAA", "VAAA|VAVA"]
OWN = "AAAV"
ROAD = "PLLL"
ORDER = [1, 2, 0, 3]
EARLY = 1
SPLIT = [16, 16, 16, 16]
QUART = {1: "VAVA", 3: "VAVA"}
SELF = [33]
STEPS = "k1 k2 k3 x04 o g0 g1 g2 g3 u01:0123:AVVA s a u22:0123:AVVA u33:0123:AVVA u44:0123:AVVA u55:0123 c0V c1 p1 c2V c3 p2 p0 t0 p3 e0 H0 l1 h1 q1 m1 l2 h2 q2 q0 m2 y1 m0 y2 l3 q3 h3 y0 z3"


def each(words):
    return words.replace("|", " ").split()


GROUPS = [words for b in BATCH for words in b.split("|")]
WIDE = [max(128, CAPP * len(each(b))) for b in BATCH]
LS = 4 * LW
GAP = 128 - CAPP
TILES = [(o, m) for o in ORDER for m in range(4 if ROAD[o] == "R" else 1)]
CALLS = [("l", c) for c in LISTS] + [(c[0], c[2:]) for calls in AFTER for c in calls.split(", ")]
HANDS = [(kind, c) for kind, c in CALLS if any(kind + w in VIA for w in each(c))]
SQ = S // 16

SCRATCH = {
    "w32": ("sbuf", [128, N * LW], "int32"),
    "w16": ("sbuf", [128, N * LW], "uint16"),
    "lst": ("sbuf", [128, LS * len(GROUPS)], "uint16"),
    "s32": ("sbuf", [128, SQ + SQ // 4], "int32"),
    "s16": ("sbuf", [128, SQ + SQ // 4], "uint16"),
    "vt": ("sbuf", [128, 4 * NV], "bfloat16"),
    "at": ("sbuf", [128, 4 * NA], "bfloat16"),
    "aq": ("sbuf", [128, NA], "float8_e4m3fn_x4"),
    "ap": ("sbuf", [128, NA], "uint8"),
    "mP": ("sbuf", [128, 128], "bfloat16"),
    "mL": ("sbuf", [128, 128], "bfloat16"),
    "mR": ("sbuf", [128, 128], "bfloat16"),
    "onef": ("sbuf", [128, 128], "float32"),
    "et": ("sbuf", [128, 512 * len(TILES)], "bfloat16"),
    "eq": ("sbuf", [128, 128 * len(TILES)], "float8_e4m3fn_x4"),
    "ep": ("sbuf", [128, 128 * len(TILES)], "uint8"),
    "ident": ("sbuf", [128, 128], "float32"),
    "xo": ("sbuf", [128, 512], "bfloat16"),
    "cq": ("sbuf", [128, W + GAP], "float8_e4m3fn_x4"),
    "cp": ("sbuf", [128, W + GAP], "uint8"),
    "dw": ("sbuf", [128, W * len(TILES)], "bfloat16"),
    "gt": ("sbuf", [128, 4 * S], "float32"),
    "gl": ("sbuf", [128, 4 * S], "bfloat16"),
    "gm": ("sbuf", [128, 4 * S], "bfloat16"),
    "ht": ("sbuf", [128, 4 * S], "bfloat16"),
    "hq": ("sbuf", [128, S], "float8_e4m3fn_x4"),
    "hp": ("sbuf", [128, S], "uint8"),
    "yt": ("sbuf", [128, 4 * NA], "float32"),
    "ps": ("psum", [128, 4096], "float32"),
}
for _i, _n in enumerate(WIDE):
    SCRATCH["x%d" % _i] = ("sbuf", [128, 4 * _n], "bfloat16")
    SCRATCH["q%d" % _i] = ("sbuf", [128, _n], "float8_e4m3fn_x4")
    SCRATCH["p%d" % _i] = ("sbuf", [128, _n], "uint8")
NEV = 100
SEMAPHORES = (["loc"] + ["via%d" % k for k in range(len(HANDS))] + ["lst%d" % i for i in range(len(GROUPS))]
              + ["arr%d" % i for i in range(len(RUNS))] + ["made%d" % k for k in range(8)] + ["free%d" % k for k in range(8)]
              + ["e%d" % k for k in range(NEV)])


KIN = {}


def learn(topo, cores):
    for r in range(N):
        far = []
        for k in range(N // 2):
            pair = (r // 2 + k) % (N // 2)
            a, b = topo.chip(cores[r]), topo.chip(cores[2 * pair])
            if a == b:
                KIN[r, "n"] = pair
            elif topo.same_plane(a, b):
                KIN[r, "p"] = pair
            else:
                far.append(pair)
        KIN[r, "f"], KIN[r, "g"] = far


def named(r, words):
    return [2 * KIN[r, w[0]] + (r + int(w[1])) % 2 for w in each(words)]


def asked(r, words):
    return [q for w in each(words) for q in range(N) if named(q, w) == [r]]


def other(r, kind, w):
    return (asked if kind == "l" else named)(r, w)[0]


def helper(topo, cores, r):
    can = [c for c in topo.cores_of(cores[r]) if topo.die(c) != topo.die(cores[r]) and all(topo.may_write(c, d) for d in cores)]
    return can[r % 2]


def shares(eng, n):
    wide, k = [1] * n, 0
    while n and sum(wide) + wide[k] <= len(eng):
        wide[k] *= 2
        k = (k + 1) % n
    return [eng[sum(wide[:k]):sum(wide[:k + 1])] for k in range(n)]


def lanes(topo, cores, r, kind, words):
    out = topo.engines(cores[r], cores[named(r, "p0")[0]])
    rest = [e for e in topo.engines(cores[r], cores[named(r, "n1")[0]]) if e not in out]
    near = [w for w in each(words) if w[0] == "n" or kind + w in VIA]
    off = [w for w in each(words) if w not in near]
    if kind == "l":
        done = [w for call in LISTS for w in each(call) if w[0] == "n" or kind + w in VIA]
        on = [rest[LNEAR * done.index(w) % len(rest):][:LNEAR] for w in near]
    else:
        on = shares(rest, len(near))
    return dict(zip(off + near, shares(out, len(off)) + on))


def handed(topo, cores, r, kind, words):
    mine = [w for w in each(words) if kind + w in VIA]
    return dict(zip(mine, shares(topo.engines(helper(topo, cores, r), cores[other(r, kind, mine[0])]), len(mine))))


def landing(topo, cores, r, kinds, words):
    n = 0
    for kind, call in CALLS:
        for w in each(call):
            if kind in kinds and w in words:
                q = (named if kind == "l" else asked)(r, w)[0]
                n += len((handed if kind + w in VIA else lanes)(topo, cores, q, kind, call)[w])
    return n


def runs(r):
    return [sorted(asked(r, words)) for words in RUNS]


def place(q, r):
    return CAPP * [x for run in runs(r) for x in run].index(q) + GAP * (q != r)


def where(T, r, kind, w):
    q = other(r, kind, w)
    if kind == "l":
        i = [w in words for words in GROUPS].index(True)
        k = LS * i + LW * each(GROUPS[i]).index(w)
        return T.w16[:, LW * q:LW * q + LW], T.w16[:, LW * q:LW * q + LW], T.lst[:, k:k + LW], T.sem["lst%d" % i]
    i = [w in b for b in BATCH].index(True)
    k, at, rest = CAPP * each(BATCH[i]).index(w), place(r, q), CAPP * q
    sem = T.sem["arr%d" % [w in words for words in RUNS].index(True)]
    if kind == "c":
        return (T["q%d" % i][:, k:k + CAPP].bitcast(dt.uint8), T.cq[:, rest:rest + CAPP].bitcast(dt.uint8),
                T.cq[:, at:at + CAPP].bitcast(dt.uint8), sem)
    return T["p%d" % i][:, k:k + CAPP], T.cp[:, rest:rest + CAPP], T.cp[:, at:at + CAPP], sem


def transfer(topo, core, eng, src, dst, sem):
    rid, pid, _ = topo.addr(core)
    return RemoteDMATransfer(dst_ids=[DstId(rid=rid, pnc=pid)], dma_engine_mask=sum(1 << e for e in eng), src=src, dst=dst,
                             remote_sem=sem)


def hand_on(g, T, topo, cores, r):
    sent = 0
    for j, (kind, call) in enumerate(HANDS):
        g.wait_ge(T.sem["via%d" % j], sum(len(e) for w, e in lanes(topo, cores, r, kind, call).items() if kind + w in VIA))
        tr = []
        for w, eng in handed(topo, cores, r, kind, call).items():
            _, rest, dst, sem = where(T, r, kind, w)
            tr.append(transfer(topo, cores[other(r, kind, w)], eng, rest, dst, sem))
            sent += len(eng)
        g.remote_dma_fused(tr, local_sem=T.sem.loc)
    g.wait_ge(T.sem.loc, sent)


def rank_program(g, core, T, topo):
    cores = list(T.cores)
    learn(topo, cores)
    r = T.rank_of(core)
    if r is None:
        for q in range(N):
            if core == helper(topo, cores, q):
                hand_on(g, T, topo, cores, q)
        return
    V, A, P, Y = g.vector, g.scalar, g.tensor, g.sync
    used, nloc = [0], [0]

    def ev():
        used[0] += 1
        return T.sem["e%d" % (used[0] - 1)]

    def copy(q, out, src, sem):
        if q is V:
            V.tensor_copy(out, src).then_inc(sem, 1)
        else:
            A.activation(out, src, COPY).then_inc(sem, 1)

    def send(kind, words):
        eng, tr = lanes(topo, cores, r, kind, words), []
        for w in each(words):
            src, rest, dst, sem = where(T, r, kind, w)
            if kind + w in VIA:
                tr.append(transfer(topo, helper(topo, cores, r), eng[w], src, rest, T.sem["via%d" % HANDS.index((kind, words))]))
            else:
                tr.append(transfer(topo, cores[other(r, kind, w)], eng[w], src, dst, sem))
            nloc[0] += len(eng[w])
        g.remote_dma_fused(tr, local_sem=T.sem.loc)

    e_w, e_v, e_s, e_a = ev(), ev(), ev(), ev()
    for k in range(4):
        (Y if k % 2 == 0 else A).dma_start(T.w32[16 * k:16 * k + 16, :], T.want[:]).then_inc(e_w, 16)
    Y.dma_start(T.vt[:], T.v[:]).then_inc(e_v, 16)
    Y.dma_start(T.at[:], T.a[:]).then_inc(e_a, 16)
    for k in range(8):
        Y.dma_start(T.s32[16 * k:16 * k + 16, 0:SQ], T.slot[:]).then_inc(e_s, 16)
    for k in range(8 * ("R" in ROAD)):
        Y.dma_start(T.s32[16 * k:16 * k + 16, SQ:SQ + 8], T.slot[:, 8 * (k // 2):8 * (k // 2) + 8]).then_inc(e_s, 16)

    e_z, e_c, e_id, e_one = (ev() for _ in range(4))
    e_m = {road: ev() for road in "LPR"}
    e_e, e_eq = [ev() for _ in TILES], {}

    def onehot(j):
        o, m = TILES[j]
        V.wait_ge(e_m[ROAD[o]], 1)
        for t in range(4):
            V.tensor_scalar(T.et[:, 512 * j + t:512 * j + 512:4], T["m" + ROAD[o]][:], 240.0 - 128 * o - 32 * m + t, None,
                            AluOpType.is_equal).then_inc(e_e[j], 1)

    def pack(a, b):
        e = ev()
        for j in range(a, b):
            V.wait_ge(e_e[j], 4)
            e_eq[j] = e
        V.quantize_mx(T.eq[:, 128 * a:128 * b], T.ep[:, 128 * a:128 * b], T.et[:, 512 * a:512 * b]).then_inc(e, 1)

    for road, pattern in (("L", [[1, 32], [32, 4]]), ("P", [[1, 128]]), ("R", [[0, 4], [1, 32]])):
        if road in ROAD:
            g.iota(T["m" + road][:], pattern, 240, -4, allow_small_or_imprecise_dtypes=True).then_inc(e_m[road], 1)
    narrow = [T.xo] + [T["x%d" % i] for i, b in enumerate(BATCH) if len(each(b)) == 1]
    for x in narrow:
        V.memset(x[:, 4 * CAPP:512], 0.0).then_inc(e_z, 1)
    if "P" in ROAD:
        V.memset(T.onef[:], 1.0).then_inc(e_one, 1)
    for j in range(EARLY):
        onehot(j)

    V.wait_ge(e_w, 64)
    for h in range(2):
        V.tensor_scalar(T.w16[64 * h:64 * h + 64, :], T.w32[0:64, :], 0.0, 4.0, AluOpType.max, AluOpType.mult).then_inc(e_c, 1)
    g.wait_ge(e_c, 2)
    for call in LISTS:
        send("l", call)
    V.wait_ge(e_z, len(narrow))
    e_own, e_s16, e_aq = ev(), ev(), ev()

    def own():
        e = ev()
        for q in (V, A):
            q.wait_ge(e_c, 2)
            q.wait_ge(e_v, 16)
        for t in range(4):
            copy(V if OWN[t] == "V" else A, T.xo[:, t:4 * CAPP:4], T.vt[:, t:4 * NV].indirect(T.w16[:, LW * r:LW * r + LW]), e)
        V.wait_ge(e, 4)
        V.quantize_mx(T.cq[:, 0:128], T.cp[:, 0:128], T.xo[:]).then_inc(e_own, 1)

    def serve(i):
        x, qb, pb = (T["%s%d" % (c, i)] for c in "xqp")
        e_g, e_q = ev(), ev()
        lo = 0
        for words, who in zip(BATCH[i].split("|"), GATHER[i].split("|")):
            k, n = GROUPS.index(words), len(each(words))
            for q in (V, A):
                q.wait_ge(T.sem["lst%d" % k], landing(topo, cores, r, "l", words))
            for t in range(4):
                copy(V if who[t] == "V" else A, x[:, 4 * CAPP * lo + t:4 * CAPP * (lo + n):4],
                     T.vt[:, t:4 * NV].indirect(T.lst[:, LS * k:LS * k + LW * n]), e_g)
            lo += n
        V.wait_ge(e_g, 4 * len(BATCH[i].split("|")))
        V.quantize_mx(qb[:], pb[:], x[:]).then_inc(e_q, 1)
        g.wait_ge(e_q, 1)
        for call in AFTER[i].split(", "):
            send(call[0], call[2:])
        if i + 1 == len(BATCH):
            if "P" in ROAD:
                g.wait_ge(e_one, 1)
                g.affine_select(T.ident[:], T.onef[:], [[-1, 128]], AluOpType.is_equal, 0.0, 0, 1).then_inc(e_id, 1)
            g.wait_ge(T.sem.loc, nloc[0])

    def slots():
        n = SQ + 8 * ("R" in ROAD)
        V.wait_ge(e_s, 128 + 128 * ("R" in ROAD))
        V.tensor_copy(T.s16[:, 0:n], T.s32[:, 0:n]).then_inc(e_s16, 1)

    def quant_a():
        V.wait_ge(e_a, 16)
        V.quantize_mx(T.aq[:], T.ap[:], T.at[:]).then_inc(e_aq, 1)

    idle, made, free, seen = list(range(8)), [0] * 8, [0] * 8, {}

    def wait(q, sem, n):
        name = "V" if q is V else "A" if q is A else "P"
        if seen.get((name, sem), 0) < n:
            q.wait_ge(T.sem[sem], n)
            seen[name, sem] = n

    def take():
        b = idle.pop(0)
        wait(P, "free%d" % b, free[b])
        made[b] += 1
        return b

    def drain(q, b, n, out, lo, hi):
        wait(q, "made%d" % b, n)
        copy(q, out, T.ps[:, 512 * b + lo:512 * b + hi], T.sem["free%d" % b])
        free[b] += 1
        if b not in idle:
            idle.append(b)
        return "free%d" % b, free[b]

    late, full = [], [[] for _ in TILES]

    def out_of(job, q):
        j, b, n, first, pieces = job
        for piece in pieces:
            c, d = place(piece[0], r) - first, W * j + CAPP * piece[0]
            full[j].append(drain(q, b, n, T.dw[:, d:d + CAPP * len(piece)], c, c + CAPP * len(piece)))

    def unpack(lo, hi, tiles, who):
        ranks = [q for run in runs(r)[lo:hi + 1] for q in run]
        for i in range(lo, hi + 1):
            if i == 0:
                P.wait_ge(e_own, 1)
            else:
                wait(P, "arr%d" % i, landing(topo, cores, r, "cs", RUNS[i]))
        end = max(128, place(ranks[-1], r) + CAPP)
        first = min(place(ranks[0], r), end - 128)
        pieces = [ranks[:1]]
        for q in ranks[1:]:
            if q == pieces[-1][-1] + 1 and pieces[-1][-1] != r:
                pieces[-1].append(q)
            else:
                pieces.append([q])
        for k, j in enumerate(tiles):
            if e_eq[j] is not None:
                P.wait_ge(e_eq[j], 1)
                e_eq[j] = None
            b = take()
            P.matmul_mx(T.ps[:, 512 * b:512 * b + end - first], T.eq[:, 128 * j:128 * j + 128], T.ep[:, 128 * j:128 * j + 128],
                        T.cq[:, first:end], T.cp[:, first:end], True, True).then_inc(T.sem["made%d" % b], 1)
            job = j, b, made[b], first, pieces
            if k < len(who):
                out_of(job, V if who[k] == "V" else A)
            else:
                late.append(job)

    e_p, e_fv, e_fa, e_h, e_hq = ([ev() for _ in range(4)] for _ in range(5))
    e_out = ev()
    nout = [0]

    def store(q, out, src):
        q.dma_start(out, src).then_inc(e_out, 16)
        nout[0] += 16

    def window(q, j, lo, hi):
        q.wait_ge(e_s16, 1)
        for sem, n in full[j][::-1]:
            wait(q, sem, n)
        return T.dw[:, W * j:W * j + W].indirect(T.s16[:, lo:hi])

    def fold(o, a, q):
        q.dma_start(T.gm[32 * a:32 * a + 32, S * o:S * o + S],
                    T.gl[:, S * o + 128 * a:S * o + 128 * a + 128]).then_inc(e_p[o], 16)

    def pick(o):
        to, j, cut = T.gt if ROAD[o] == "P" else T.gl, TILES.index((o, 0)), SPLIT[o]
        if ROAD[o] == "R":
            for m in range(4):
                q = V if QUART[o][m] == "V" else A
                copy(q, T.gm[:, S * o + 128 * m:S * o + 128 * m + 128], window(q, j + m, SQ, SQ + 8), e_p[o])
            return
        if o in QUART:
            e4 = [ev() for _ in range(4)]
            for a in range(4):
                q = V if QUART[o][a] == "V" else A
                copy(q, to[:, S * o + 128 * a:S * o + 128 * a + 128], window(q, j, 8 * a, 8 * a + 8), e4[a])
            for a in range(4):
                q = A if 10 * o + a in SELF else Y
                q.wait_ge(e4[a], 1)
                fold(o, a, q)
            return
        for q, lo, hi, e in ((V, 0, cut, e_fv[o]), (A, cut, SQ, e_fa[o])):
            copy(q, to[:, S * o + 16 * lo:S * o + 16 * hi], window(q, j, lo, hi), e)
        for a in range(4 * (ROAD[o] == "L")):
            q = A if 10 * o + a in SELF else Y
            if 8 * a < cut:
                q.wait_ge(e_fv[o], 1)
            if 8 * a + 8 > cut:
                q.wait_ge(e_fa[o], 1)
            fold(o, a, q)

    held, done = {}, {o: [] for o in range(4)}

    def turn(o):
        P.wait_ge(e_id, 1)
        P.wait_ge(e_fv[o], 1)
        P.wait_ge(e_fa[o], 1)
        held[o] = []
        for t in range(4):
            b = take()
            P.transpose(T.ps[:, 512 * b:512 * b + 128], T.gt[:, S * o + t:S * o + S:4], T.ident[:]).then_inc(T.sem["made%d" % b], 1)
            held[o].append((b, made[b]))

    def empty(o, q):
        for t, (b, n) in enumerate(held[o]):
            done[o].append(drain(q, b, n, T.ht[:, 512 * o + t:512 * o + 512:4], 0, 128))

    def turn_here(o):
        V.wait_ge(e_p[o], 4 if ROAD[o] == "R" else 64)
        for t in range(4):
            V.transpose(T.ht[:, 512 * o + t:512 * o + 512:4], T.gm[:, S * o + t:S * o + S:4]).then_inc(e_h[o], 1)

    def turned(q, o):
        if ROAD[o] != "P":
            q.wait_ge(e_h[o], 4)
        for sem, n in done[o]:
            q.wait_ge(T.sem[sem], n)

    def quant(o):
        turned(V, o)
        V.quantize_mx(T.hq[:, 128 * o:128 * o + 128], T.hp[:, 128 * o:128 * o + 128],
                      T.ht[:, 512 * o:512 * o + 512]).then_inc(e_hq[o], 1)

    def h_out(o, q=Y):
        turned(q, o)
        store(q, T.h[:, 512 * o:512 * o + 512], T.ht[:, 512 * o:512 * o + 512])

    def product(o, lo=0, hi=NA):
        P.wait_ge(e_aq, 1)
        P.wait_ge(e_hq[o], 1)
        b = take()
        P.matmul_mx(T.ps[:, 512 * b:512 * b + hi - lo], T.hq[:, 128 * o:128 * o + 128], T.hp[:, 128 * o:128 * o + 128],
                    T.aq[:, lo:hi], T.ap[:, lo:hi], True, True).then_inc(T.sem["made%d" % b], 1)
        held[o] = b, made[b]

    def y_out(o, q, d=Y, lo=0, hi=NA):
        sem, n = drain(q, *held[o], T.yt[:, NA * o + lo:NA * o + hi], 0, hi - lo)
        d.wait_ge(T.sem[sem], n)
        store(d, T.y[:, NA * o + lo:NA * o + hi], T.yt[:, NA * o + lo:NA * o + hi])

    def last(o):
        for h, q, d in ((0, V, Y), (1, A, A)):
            product(o, 128 * h, 128 * h + 128)
            y_out(o, q, d, 128 * h, 128 * h + 128)

    step = {"p": pick, "l": turn_here, "q": quant, "m": product, "y": y_out, "h": h_out, "z": last, "e": empty, "k": onehot,
            "c": lambda k, q: out_of(late[k], q), "H": lambda o: h_out(o, A), "t": turn, "g": serve}
    for w in STEPS.split():
        if w in "aso":
            {"a": quant_a, "s": slots, "o": own}[w]()
        elif w[0] == "x":
            pack(int(w[1]), int(w[2]))
        elif w[0] == "u":
            unpack(int(w[1]), int(w[2]), [int(j) for j in w.split(":")[1]], w.split(":")[2] if w.count(":") > 1 else "")
        elif w[0] in "yce":
            step[w[0]](int(w[1]), V if w[2:] == "V" else A)
        else:
            step[w[0]](int(w[1]))
    Y.wait_ge(e_out, nout[0])
